import numpy as np
import ml_dtypes


def mxq(x, axis, fmt="e4m3"):
    dtype, down = {"e4m3": (ml_dtypes.float8_e4m3fn, 7), "e5m2": (ml_dtypes.float8_e5m2, 14)}[fmt]
    v = np.moveaxis(np.asarray(x, np.float32).astype(ml_dtypes.bfloat16).astype(np.float64), axis, -1)
    blocks = v.reshape(v.shape[:-1] + (-1, 32))
    amax = np.abs(blocks).max(-1, keepdims=True)
    byte = np.maximum(np.where(amax > 0, np.frexp(amax)[1] - 1 + 127, 0) - down, 1)
    scale = np.exp2(byte - 127.0)
    codes = (blocks / scale).astype(np.float32).astype(dtype).astype(np.float64)
    return np.moveaxis((codes * scale).reshape(v.shape), -1, axis)


WIDE = False


def mx_kscale(k):
    if not WIDE:
        return np.ones(k)
    levels = np.array([10, -10, 5, -5, 0])
    if k % 512:
        return np.exp2(np.random.permutation(np.resize(levels, k // 32))).repeat(32)
    a = np.empty((k // 512, 16))
    for p in range(k // 512):
        a[p, :8] = np.random.permutation(np.resize(levels, 8))
        for g in range(8):
            far = levels[np.abs(levels - a[p, g]) >= 10]
            a[p, g + 8] = far[np.random.randint(len(far))]
    return np.exp2(a.ravel()).repeat(32)


def f64(x):
    return np.asarray(x).astype(np.float64)


def striped(idx):
    return np.tile(idx.reshape(-1, 16).T, (8, 1)).astype(np.uint16)


def unstriped(offs):
    return offs[:16].T.reshape(-1).astype(np.int64)


def striped8(idx):
    return np.concatenate([x.reshape(-1, 16).T for x in idx]).astype(np.uint16)


def runs(offs, k):
    lists = np.stack([offs[16 * r : 16 * r + 16].T.reshape(-1) for r in range(8)]).astype(np.int64)
    return lists[np.arange(k) % 512 // 64]


def pack_weight(w):
    k, n = w.shape
    w = f64(np.asarray(w, np.float32).astype(ml_dtypes.bfloat16)).reshape(k // 32, 32, n)
    amax = np.abs(w).max(1)
    byte = np.clip(np.where(amax > 0, np.frexp(amax)[1] - 1 + 127 - 7, 1), 1, 254)
    scaled = (w * np.exp2(127.0 - byte)[:, None, :]).reshape(k, n).astype(np.float32)
    words = np.ascontiguousarray(scaled.reshape(k // 512, 128, 4, n).transpose(0, 1, 3, 2)).astype(ml_dtypes.float8_e4m3fn).view(np.uint8)
    return words, np.ascontiguousarray(byte.astype(np.uint8).reshape(k // 512, 16, n))


def unpack_weight(words, scales):
    g, p, n, _ = words.shape
    vals = np.ascontiguousarray(words).view(ml_dtypes.float8_e4m3fn).astype(np.float64) * np.repeat(np.exp2(scales.astype(np.float64) - 127.0), 8, axis=1)[..., None]
    return vals.transpose(0, 1, 3, 2).reshape(g * 512, n)

def planes(y):
    n, m = y.shape
    v = y.astype(np.float32).astype(ml_dtypes.bfloat16).astype(np.float64).reshape(n // 32, 32, m)
    top = np.abs(v).max(1)
    byte = np.clip(np.where(top > 0, np.frexp(top)[1] - 1 + 127 - 7, 1), 1, 254)
    codes = (v * np.exp2(127.0 - byte)[:, None, :]).reshape(n, m).astype(np.float32).astype(ml_dtypes.float8_e4m3fn).view(np.uint8)
    words = codes.reshape(n // 512, 128, 4, m).transpose(0, 1, 3, 2)
    return np.ascontiguousarray(words), np.ascontiguousarray(byte.astype(np.uint8).reshape(n // 512, 16, m))


K, T, S, N, H = 512, 2048, 512, 512, 512


def setup_inputs():
    n = np.random.standard_normal
    s = mx_kscale(K)[:, None]
    u = mx_kscale(H)
    packed_xT = pack_weight(n((K, T)) * s)
    packed_w1 = pack_weight(n((K, H)) / np.sqrt(K) / s)
    packed_w2 = pack_weight(n((H, H)) / np.sqrt(H) / u[:, None])
    packed_w3 = pack_weight(n((H, N)) / np.sqrt(H) / u[:, None])
    return {
        "x_words": packed_xT[0],
        "x_scales": packed_xT[1],
        "w1_words": packed_w1[0],
        "w1_scales": packed_w1[1],
        "gn": (np.random.uniform(0.5, 1.5, (H, 1)) * u[:, None]).astype(np.float32),
        "w2_words": packed_w2[0],
        "w2_scales": packed_w2[1],
        "res": n((N, S)).astype(np.float32),
        "w3_words": packed_w3[0],
        "w3_scales": packed_w3[1],
        "offs": striped(np.random.permutation(T)[:S]),
        "p1": striped8(np.stack([np.random.permutation(S) for _ in range(8)])),
        "p2": striped8(np.stack([np.random.permutation(S) for _ in range(8)])),
        "p3": striped8(np.stack([np.random.permutation(S) for _ in range(8)])),
        "mv": striped8(np.stack([np.random.permutation(S) for _ in range(8)])),
    }


def reference(x_words, x_scales, w1_words, w1_scales, gn, w2_words, w2_scales, res, w3_words, w3_scales, offs, p1, p2, p3, mv):
    xq = unpack_weight(x_words, x_scales)[:, unstriped(offs)]
    y = unpack_weight(w1_words, w1_scales).T @ xq
    x1 = y[np.arange(H)[:, None], runs(p1, H)]
    r1 = x1 / ((x1 - y) ** 2 + 1)
    x2 = y[np.arange(H)[:, None], runs(p2, H)]
    r2 = x2 / ((x2 - y) ** 2 + 1)
    x3 = y[np.arange(H)[:, None], runs(p3, H)]
    r3 = x3 / ((x3 - y) ** 2 + 1)
    z = f64(gn) * (r1 + r2 + r3)
    h = np.tanh(unpack_weight(w2_words, w2_scales).T @ mxq(z, 0, "e4m3"))
    z2 = f64(gn) * (h[np.arange(H)[:, None], runs(mv, H)])
    out_0 = f64(res) + (unpack_weight(w3_words, w3_scales).T @ mxq(z2, 0, "e4m3"))
    return (out_0,) + planes(out_0)

@@ -1,0 +1,337 @@
+from contextlib import ExitStack
+
+import concourse.mybir as mybir
+from concourse.masks import make_identity
+
+F32 = mybir.dt.float32
+BF16 = mybir.dt.bfloat16
+I32 = mybir.dt.int32
+U32 = mybir.dt.uint32
+U16 = mybir.dt.uint16
+U8 = mybir.dt.uint8
+FP8X4 = mybir.dt.float8_e4m3fn_x4
+ACT = mybir.ActivationFunctionType
+ALU = mybir.AluOpType
+
+P = 128
+T = 2048
+S = 512
+FLOPS = 3 * 2 * 512 * 512 * 512
+
+CHUNKS1 = [(0, 256), (256, 384), (384, 512)]
+XB = 3
+GB = 4
+SQB = 1
+LAG = 2
+CHUNKS2 = [(0, 128), (128, 256), (256, 384), (384, 512)]
+
+
+def tile_picked_irls8_none_po_kernel(
+    tc, x_words, x_scales, w1_words, w1_scales, gn, w2_words, w2_scales, res, w3_words, w3_scales,
+    offs, p1, p2, p3, mv, out_0, out_1, out_2,
+):
+    nc = tc.nc
+    with ExitStack() as ctx:
+        keep = ctx.enter_context(tc.tile_pool(name="keep", bufs=1))
+        ring = ctx.enter_context(tc.tile_pool(name="ring", bufs=3))
+        psum = ctx.enter_context(tc.psum_pool(name="psum", bufs=1))
+
+        def words_view(w):
+            return w[0].rearrange("p n t -> p (n t)").bitcast(I32)
+
+        def load_scales(plane, scales, row, quadrants):
+            for q in quadrants:
+                nc.sync.dma_start(out=plane[32 * q + row : 32 * q + row + 4, :].bitcast(I32), in_=scales[0, 4 * q : 4 * q + 4, :].bitcast(I32))
+
+        offs_t = keep.tile([P, S // 16], U16, name="offs_t")
+        lists = [keep.tile([P, S // 16], U16, name="list%d" % i) for i in range(4)]
+        xw = keep.tile([P, T], I32, name="xw", align_bytes=64)
+        xs = keep.tile([P, T], U8, name="xs", align_bytes=64)
+        w_raw = [keep.tile([P, S], I32, name="w_raw%d" % i, align_bytes=64) for i in range(3)]
+        s_raw = [keep.tile([P, S], U8, name="s_raw%d" % i, align_bytes=64) for i in range(2)]
+        wq = [keep.tile([P, S], I32, name="wq%d" % i, align_bytes=64) for i in range(3)]
+        ws = [keep.tile([P, S], U8, name="ws%d" % i, align_bytes=64) for i in range(2)]
+        gain = keep.tile([P, 4], F32, name="gain")
+        resid = keep.tile([P, 4, S], F32, name="resid")
+        warm = keep.tile([P, 2], F32, name="warm")
+
+        ident = keep.tile([P, P], F32, name="ident")
+        nc.vector.memset(xs[:].bitcast(I32), 0)
+        nc.gpsimd.memset(s_raw[0][:].bitcast(I32), 0)
+        nc.gpsimd.memset(warm[:, 0:1], 1.0)
+        nc.scalar.activation(out=warm[:, 1:2], in_=warm[:, 0:1], func=ACT.Abs_reciprocal_sqrt)
+        nc.gpsimd.memset(s_raw[1][:].bitcast(I32), 0)
+        make_identity(nc, ident[:])
+
+        nc.sync.dma_start(offs_t[:], offs)
+        nc.sync.dma_start(out=w_raw[0][:], in_=words_view(w1_words))
+        load_scales(xs, x_scales, 0, range(4))
+        nc.sync.dma_start(out=xw[:], in_=words_view(x_words))
+        load_scales(s_raw[0], w1_scales, 0, range(4))
+        for tile_, src in zip(lists[:3], (p1, p2, p3)):
+            nc.sync.dma_start(tile_[:], src)
+        nc.sync.dma_start(out=gain[:], in_=gn.rearrange("(p t) o -> p (t o)", t=4))
+        nc.sync.dma_start(out=w_raw[1][:], in_=words_view(w2_words))
+        nc.sync.dma_start(out=w_raw[2][:], in_=words_view(w3_words))
+        load_scales(s_raw[1], w2_scales, 0, range(4))
+        load_scales(s_raw[1], w3_scales, 4, range(4))
+        nc.sync.dma_start(lists[3][:], mv)
+        nc.sync.dma_start(out=resid[:], in_=res.rearrange("(p t) s -> p t s", t=4))
+
+        def deal(dst, src):
+            nc.vector.tensor_copy(out=dst[:].rearrange("p (t m) -> p m t", t=4), in_=src[:].rearrange("p (m t) -> p m t", t=4))
+
+        def product(bank, i, t, codes, scales, lo, hi):
+            m = slice(P * t, P * (t + 1))
+            plane = (ws[0][:, m], ws[1][:, m], ws[1][4:P, m])[i]
+            nc.tensor.matmul_mx(out=bank[:, lo:hi], lhsT=wq[i][:, m].bitcast(FP8X4), lhsT_scale=plane,
+                                rhs=codes.bitcast(FP8X4), rhs_scale=scales, start=True, stop=True)
+
+        deal(wq[0], w_raw[0])
+        deal(ws[0], s_raw[0])
+        ybank = [psum.tile([P, S], F32, name="ybank%d" % t, tag="a%d" % t) for t in range(4)]
+        picked = []
+        ps = keep.tile([P, S], U8, name="ps", align_bytes=64)
+        nc.vector.tensor_copy(out=ps[:], in_=xs[:].indirect(offs_t[:]))
+        for lo, hi in ((0, 256), (256, 512)):
+            pw = keep.tile([P, hi - lo], U32, name="pw%d" % lo, align_bytes=64)
+            nc.vector.tensor_copy(out=pw[:], in_=xw[:].bitcast(U32).indirect(offs_t[:, lo // 16 : hi // 16]))
+            picked.append((pw, lo, hi))
+        y = [keep.tile([P, S], F32, name="y%d" % t) for t in range(4)]
+        for t in range(4):
+            for pw, lo, hi in picked:
+                product(ybank[t], 0, t, pw[:], ps[:, lo:hi], lo, hi)
+            nc.scalar.copy(out=y[t][:], in_=ybank[t][:])
+        deal(wq[1], w_raw[1])
+        deal(ws[1], s_raw[1])
+        deal(wq[2], w_raw[2])
+
+        units = [(c, t) for c in range(len(CHUNKS1)) for t in range(4)]
+        last = len(CHUNKS1) - 1
+        r_last = keep.tile([P, 3, 4, P], F32, name="r_last")
+        sums = {}
+        xg = {}
+        wt = {}
+
+        def front(c, t):
+            lo, hi = CHUNKS1[c]
+            n = hi - lo
+            u = 4 * c + t
+            x01 = ring.tile([P, 2, n], F32, name="x01", tag="x01", bufs=XB, align_bytes=64)
+            x2 = ring.tile([P, n], F32, name="x2", tag="x2", bufs=XB)
+            for k, dst in enumerate((x01[:, 0, :], x01[:, 1, :], x2[:])):
+                nc.vector.tensor_copy(out=dst, in_=y[t][:].indirect(lists[k][:, lo // 16 : hi // 16]))
+            d = keep.tile([P, 3, n], F32, name="d%d" % u)
+            nc.vector.tensor_tensor(out=d[:, 0:2, :], in0=x01[:], in1=y[t][:, lo:hi].unsqueeze(1).to_broadcast([P, 2, n]), op=ALU.subtract)
+            nc.vector.tensor_tensor(out=d[:, 2, :], in0=x2[:], in1=y[t][:, lo:hi], op=ALU.subtract)
+            w = keep.tile([P, 3, n], F32, name="w%d" % u)
+            flat_d = d[:].rearrange("p k n -> p (k n)")
+            flat_w = w[:].rearrange("p k n -> p (k n)")
+            parts = (slice(0, 2 * n), slice(2 * n, 3 * n))
+            sq = [ring.tile([P, s.stop - s.start], F32, name="sq", tag="sq%d" % i, bufs=SQB) for i, s in enumerate(parts)]
+            for i, s in enumerate(parts):
+                nc.scalar.activation(out=sq[i][:], in_=flat_d[:, s], func=ACT.Square)
+            q = ring.tile([P, 3 * n], F32, name="q", tag="q")
+            for i, s in enumerate(parts):
+                nc.scalar.activation(out=q[:, s], in_=sq[i][:], func=ACT.Abs_reciprocal_sqrt, bias=1.0)
+            for s in parts:
+                nc.scalar.activation(out=flat_w[:, s], in_=q[:, s], func=ACT.Square)
+            xg[c, t] = (x01, x2)
+            wt[c, t] = w
+
+        def back(c, t):
+            lo, hi = CHUNKS1[c]
+            if c == last:
+                r = r_last[:, :, t, :]
+            else:
+                r_tile = ring.tile([P, 3, hi - lo], F32, name="r", tag="r")
+                r = r_tile[:]
+            x01, x2 = xg[c, t]
+            g = gain[:, t : t + 1]
+            nc.vector.scalar_tensor_tensor(out=r[:, 0:2, :], in0=x01[:], scalar=g, in1=wt[c, t][:, 0:2, :], op0=ALU.mult, op1=ALU.mult)
+            nc.vector.scalar_tensor_tensor(out=r[:, 2, :], in0=x2[:], scalar=g, in1=wt[c, t][:, 2, :], op0=ALU.mult, op1=ALU.mult)
+            if c == last:
+                return
+            for j in range(lo, hi, P):
+                if t == 0:
+                    sums[j] = psum.tile([P, S], F32, name="sums", tag="a%d" % (j // P % 2))
+                for k in range(3):
+                    nc.tensor.matmul(out=sums[j][:, P * t : P * (t + 1)], lhsT=r[:, k, j - lo : j - lo + P], rhs=ident[:],
+                                     start=(k == 0), stop=(k == 2), is_transpose=True)
+            if t == 3:
+                finish(c)
+
+        def quantise(planes, n, tag, late=False):
+            if late:
+                zq = ring.tile([P, n], U32, name="zq", tag="x01", bufs=XB, align_bytes=64)
+            else:
+                zq = keep.tile([P, n], U32, name="q" + tag, align_bytes=64)
+            zs = keep.tile([P, n], U8, name="s" + tag, align_bytes=64)
+            nc.vector.quantize_mx(out=zq[:].bitcast(FP8X4), scales=zs[:], in_=planes[:].rearrange("p n t -> p (n t)"))
+            return zq, zs
+
+        gain2 = keep.tile([P, 4], F32, name="gain2")
+        nc.vector.tensor_scalar(out=gain2[:], in0=gain[:], scalar1=2.0, scalar2=None, op0=ALU.mult)
+        window = [keep.tile([P, S], F32, name="window%d" % t) for t in range(4)]
+        u_tags = (("b0", "b0", "b1", "b1"), ("b2", "b2", "b2", "b2"), ("b3", "a0", "a1", "a2"))
+        upre = {}
+        rounded = {}
+        sigs = {}
+
+        def second_product(zb, c):
+            lo, hi = CHUNKS1[c]
+            n = hi - lo
+            zq, zs = quantise(zb, n, "z%d" % lo, c < last)
+            banks = {}
+            for t in range(4):
+                tag = u_tags[c][t]
+                place = u_tags[c][:t].count(tag) * n
+                if tag not in banks:
+                    banks[tag] = psum.tile([P, S], F32, name="ubank", tag=tag)
+                product(banks[tag], 1, t, zq[:], zs[:], place, place + n)
+                upre[c, t] = banks[tag][:, place : place + n]
+            if c < last:
+                upre[c, "01"] = banks[u_tags[c][0]][:, 0 : 2 * n]
+
+        def doubled(c):
+            lo, hi = CHUNKS1[c]
+            for t in (2, 3):
+                if c == last:
+                    nc.scalar.activation(out=window[t][:, lo:hi], in_=upre[c, t], func=ACT.Copy, scale=2.0)
+                else:
+                    nc.vector.tensor_scalar(out=window[t][:, lo:hi], in0=upre[c, t], scalar1=2.0, scalar2=None, op0=ALU.mult)
+
+        def centre(dst, sig, t):
+            nc.vector.tensor_scalar(out=dst, in0=sig, scalar1=0.5, scalar2=gain2[:, t : t + 1], op0=ALU.subtract, op1=ALU.mult)
+
+        def squash(c):
+            lo, hi = CHUNKS1[c]
+            n = hi - lo
+            if c < last:
+                sig = ring.tile([P, 2, n], F32, name="sig_early", tag="sq%d" % c, bufs=SQB)
+                nc.scalar.activation(out=sig[:].rearrange("p t n -> p (t n)"), in_=upre[c, "01"], func=ACT.Sigmoid, scale=2.0)
+            else:
+                sig = keep.tile([P, 2, n], F32, name="sig_last")
+                for t in (0, 1):
+                    nc.scalar.activation(out=sig[:, t, :], in_=upre[c, t], func=ACT.Sigmoid, scale=2.0)
+            sigs[c] = sig
+
+        def apply_gain(c):
+            lo, hi = CHUNKS1[c]
+            for t in (0, 1):
+                centre(window[t][:, lo:hi], sigs[c][:, t, :], t)
+
+        def finish(c):
+            lo, hi = CHUNKS1[c]
+            n = hi - lo
+            zt = keep.tile([P, n // P, 2, P, 2], BF16, name="zt%d" % c, align_bytes=64)
+            for i in range(n // P):
+                nc.scalar.activation(out=zt[:, i], in_=sums[lo + i * P][:].rearrange("p (u e m) -> p u m e", u=2, e=2), func=ACT.Copy)
+            words = zt[:].rearrange("p i u m e -> p (i u m e)").bitcast(F32)
+            turned = psum.tile([P, 2 * n], F32, name="turned", tag="a%d" % (2 + c))
+            for i in range(n // P):
+                for u in range(2):
+                    nc.tensor.transpose(turned[:, u * n + i * P : u * n + (i + 1) * P], words[:, (2 * i + u) * P : (2 * i + u + 1) * P], ident[:])
+            zb = keep.tile([P, n, 4], BF16, name="zb%d" % c, align_bytes=64)
+            nc.scalar.copy(out=zb[:].rearrange("p n t -> p (n t)").bitcast(F32).rearrange("p (n u) -> p n u", u=2),
+                           in_=turned[:].rearrange("p (u n) -> p n u", u=2))
+            rounded[c] = zb
+
+        part = keep.tile([P, 4, P], F32, name="part")
+        z = keep.tile([P, 4, P], F32, name="z")
+
+        def add_up(ts):
+            nc.vector.tensor_tensor(out=part[:, ts], in0=r_last[:, 0, ts], in1=r_last[:, 1, ts], op=ALU.add)
+
+        def add_third(ts):
+            nc.vector.tensor_tensor(out=z[:, ts], in0=part[:, ts], in1=r_last[:, 2, ts], op=ALU.add)
+
+        for u, (c, t) in enumerate(units):
+            front(c, t)
+            if u >= LAG:
+                back(*units[u - LAG])
+        for c, t in units[-LAG:-1]:
+            back(c, t)
+        for c in range(last):
+            second_product(rounded[c], c)
+            squash(c)
+        add_up(slice(0, 3))
+        back(last, 3)
+        add_third(slice(0, 3))
+        add_up(slice(3, 4))
+        add_third(slice(3, 4))
+        zb_last = keep.tile([P, P, 4], BF16, name="zb_last", align_bytes=64)
+        nc.vector.tensor_copy(out=zb_last[:], in_=z[:].rearrange("p t n -> p n t"))
+        second_product(zb_last, last)
+        squash(last)
+        doubled(last)
+        for c in range(last):
+            doubled(c)
+        for c in range(last + 1):
+            apply_gain(c)
+
+        oq = keep.tile([P, S], U32, name="oq", align_bytes=64)
+        osc = keep.tile([P, S], U8, name="osc", align_bytes=64)
+        out_rows = out_0.rearrange("(p t) s -> p t s", t=4)
+        out_words = words_view(out_1)
+        stage = {}
+
+        def fetch(c):
+            lo, hi = CHUNKS2[c]
+            n = hi - lo
+            g = ring.tile([P, 4, n], BF16, name="g", tag="g", bufs=GB, align_bytes=64)
+            entries = lists[3][:, lo // 16 : hi // 16]
+            sig = ring.tile([P, 2, n], F32, name="sig", tag="sig", bufs=2)
+            for t in (2, 3):
+                nc.scalar.activation(out=sig[:, t - 2, :], in_=window[t][:].indirect(entries), func=ACT.Sigmoid)
+            for t in (0, 1):
+                nc.vector.tensor_copy(out=g[:, t, :], in_=window[t][:].indirect(entries))
+            for t in (2, 3):
+                centre(g[:, t, :], sig[:, t - 2, :], t)
+            zb = keep.tile([P, n, 4], BF16, name="z2b%d" % lo, align_bytes=64)
+            nc.scalar.activation(out=zb[:], in_=g[:].rearrange("p t n -> p n t"), func=ACT.Copy)
+            stage[c] = zb
+
+        def last_product(c):
+            lo, hi = CHUNKS2[c]
+            n = hi - lo
+            zq, zs = quantise(stage[c], n, "z2%d" % lo)
+            per_bank = S // n
+            banks = [psum.tile([P, S], F32, name="obank", tag="b%d" % c) for b in range(4 // per_bank)]
+            for t in range(4):
+                product(banks[t // per_bank], 2, t, zq[:], zs[:], (t % per_bank) * n, (t % per_bank + 1) * n)
+            stage[c] = banks
+
+        def way_out(c):
+            lo, hi = CHUNKS2[c]
+            n = hi - lo
+            per_bank = S // n
+            o = keep.tile([P, 4, n], F32, name="o%d" % lo)
+            for b, bank in enumerate(stage[c]):
+                ts = slice(b * per_bank, (b + 1) * per_bank)
+                nc.vector.tensor_tensor(out=o[:, ts, :], in0=bank[:].rearrange("p (t n) -> p t n", n=n), in1=resid[:, ts, lo:hi], op=ALU.add)
+            nc.sync.dma_start(out=out_rows[:, :, lo:hi], in_=o[:])
+            ob = keep.tile([P, n, 4], BF16, name="ob%d" % lo, align_bytes=64)
+            nc.scalar.activation(out=ob[:], in_=o[:].rearrange("p t n -> p n t"), func=ACT.Copy)
+            stage[c, "ob"] = ob
+
+        def planes_out(c):
+            lo, hi = CHUNKS2[c]
+            nc.vector.quantize_mx(out=oq[:, lo:hi].bitcast(FP8X4), scales=osc[:, lo:hi], in_=stage[c, "ob"][:].rearrange("p n t -> p (n t)"))
+            if hi >= 384:
+                first = 0 if hi == 384 else lo
+                nc.sync.dma_start(out=out_words[:, first:hi], in_=oq[:, first:hi].bitcast(I32))
+
+        for c in range(len(CHUNKS2)):
+            fetch(c)
+            if c > 0:
+                last_product(c - 1)
+        last_product(len(CHUNKS2) - 1)
+        for c in range(len(CHUNKS2)):
+            way_out(c)
+            if c > 0:
+                planes_out(c - 1)
+        planes_out(len(CHUNKS2) - 1)
+        for q in range(4):
+            queue = nc.scalar if q % 2 else nc.sync
+            queue.dma_start(out=out_2[0, 4 * q : 4 * q + 4, :].bitcast(I32), in_=osc[32 * q : 32 * q + 4, :].bitcast(I32))

@@ -19,7 +19,7 @@ S = 512
 FLOPS = 3 * 2 * 512 * 512 * 512
 
 CHUNKS1 = [(0, 256), (256, 384), (384, 512)]
-XB = 3
+XB = 5
 GB = 4
 SQB = 1
 LAG = 2
@@ -78,6 +78,17 @@ def tile_picked_irls8_none_po_kernel(
         nc.sync.dma_start(lists[3][:], mv)
         nc.sync.dma_start(out=resid[:], in_=res.rearrange("(p t) s -> p t s", t=4))
 
+        def weave_views(dst, planes):
+            return dst[:].rearrange("p (c i) t -> p c t i", i=4), planes.rearrange("p t (c i) -> p c t i", i=4)
+
+        def weave_scalar(dst, planes):
+            out, in_ = weave_views(dst, planes)
+            nc.scalar.activation(out=out, in_=in_, func=ACT.Copy)
+
+        def weave_vector(dst, planes):
+            out, in_ = weave_views(dst, planes)
+            nc.vector.tensor_copy(out=out, in_=in_)
+
         def deal(dst, src):
             nc.vector.tensor_copy(out=dst[:].rearrange("p (t m) -> p m t", t=4), in_=src[:].rearrange("p (m t) -> p m t", t=4))
 
@@ -90,6 +101,7 @@ def tile_picked_irls8_none_po_kernel(
         deal(wq[0], w_raw[0])
         deal(ws[0], s_raw[0])
         ybank = [psum.tile([P, S], F32, name="ybank%d" % t, tag="a%d" % t) for t in range(4)]
+        spare = psum.tile([P, S], F32, name="spare", tag="b0")
         picked = []
         ps = keep.tile([P, S], U8, name="ps", align_bytes=64)
         nc.vector.tensor_copy(out=ps[:], in_=xs[:].indirect(offs_t[:]))
@@ -99,9 +111,13 @@ def tile_picked_irls8_none_po_kernel(
             picked.append((pw, lo, hi))
         y = [keep.tile([P, S], F32, name="y%d" % t) for t in range(4)]
         for t in range(4):
-            for pw, lo, hi in picked:
-                product(ybank[t], 0, t, pw[:], ps[:, lo:hi], lo, hi)
-            nc.scalar.copy(out=y[t][:], in_=ybank[t][:])
+            for i, (pw, lo, hi) in enumerate(picked):
+                bank = spare if (t, i) == (0, 1) else ybank[t]
+                product(bank, 0, t, pw[:], ps[:, lo:hi], lo, hi)
+                if t == 0:
+                    nc.scalar.copy(out=y[t][:, lo:hi], in_=bank[:, lo:hi])
+            if t > 0:
+                nc.scalar.copy(out=y[t][:], in_=ybank[t][:])
         deal(wq[1], w_raw[1])
         deal(ws[1], s_raw[1])
         deal(wq[2], w_raw[2])
@@ -117,26 +133,25 @@ def tile_picked_irls8_none_po_kernel(
             lo, hi = CHUNKS1[c]
             n = hi - lo
             u = 4 * c + t
-            x01 = ring.tile([P, 2, n], F32, name="x01", tag="x01", bufs=XB, align_bytes=64)
-            x2 = ring.tile([P, n], F32, name="x2", tag="x2", bufs=XB)
-            for k, dst in enumerate((x01[:, 0, :], x01[:, 1, :], x2[:])):
-                nc.vector.tensor_copy(out=dst, in_=y[t][:].indirect(lists[k][:, lo // 16 : hi // 16]))
+            x = ring.tile([P, 3, n], F32, name="x", tag="xq", bufs=XB, align_bytes=64)
             d = keep.tile([P, 3, n], F32, name="d%d" % u)
-            nc.vector.tensor_tensor(out=d[:, 0:2, :], in0=x01[:], in1=y[t][:, lo:hi].unsqueeze(1).to_broadcast([P, 2, n]), op=ALU.subtract)
-            nc.vector.tensor_tensor(out=d[:, 2, :], in0=x2[:], in1=y[t][:, lo:hi], op=ALU.subtract)
+            for k in range(3):
+                nc.vector.tensor_copy(out=x[:, k, :], in_=y[t][:].indirect(lists[k][:, lo // 16 : hi // 16]))
+            for k in range(3):
+                nc.gpsimd.tensor_tensor(out=d[:, k, :], in0=x[:, k, :], in1=y[t][:, lo:hi], op=ALU.subtract)
             w = keep.tile([P, 3, n], F32, name="w%d" % u)
             flat_d = d[:].rearrange("p k n -> p (k n)")
             flat_w = w[:].rearrange("p k n -> p (k n)")
-            parts = (slice(0, 2 * n), slice(2 * n, 3 * n))
+            parts = (slice(0, 3 * n // 2), slice(3 * n // 2, 3 * n))
             sq = [ring.tile([P, s.stop - s.start], F32, name="sq", tag="sq%d" % i, bufs=SQB) for i, s in enumerate(parts)]
             for i, s in enumerate(parts):
                 nc.scalar.activation(out=sq[i][:], in_=flat_d[:, s], func=ACT.Square)
-            q = ring.tile([P, 3 * n], F32, name="q", tag="q")
+            q = ring.tile([P, 3 * n], F32, name="q", tag="xq", bufs=XB, align_bytes=64)
             for i, s in enumerate(parts):
                 nc.scalar.activation(out=q[:, s], in_=sq[i][:], func=ACT.Abs_reciprocal_sqrt, bias=1.0)
             for s in parts:
                 nc.scalar.activation(out=flat_w[:, s], in_=q[:, s], func=ACT.Square)
-            xg[c, t] = (x01, x2)
+            xg[c, t] = x
             wt[c, t] = w
 
         def back(c, t):
@@ -146,10 +161,7 @@ def tile_picked_irls8_none_po_kernel(
             else:
                 r_tile = ring.tile([P, 3, hi - lo], F32, name="r", tag="r")
                 r = r_tile[:]
-            x01, x2 = xg[c, t]
-            g = gain[:, t : t + 1]
-            nc.vector.scalar_tensor_tensor(out=r[:, 0:2, :], in0=x01[:], scalar=g, in1=wt[c, t][:, 0:2, :], op0=ALU.mult, op1=ALU.mult)
-            nc.vector.scalar_tensor_tensor(out=r[:, 2, :], in0=x2[:], scalar=g, in1=wt[c, t][:, 2, :], op0=ALU.mult, op1=ALU.mult)
+            nc.vector.scalar_tensor_tensor(out=r, in0=xg[c, t][:], scalar=gain[:, t : t + 1], in1=wt[c, t][:], op0=ALU.mult, op1=ALU.mult)
             if c == last:
                 return
             for j in range(lo, hi, P):
@@ -161,11 +173,8 @@ def tile_picked_irls8_none_po_kernel(
             if t == 3:
                 finish(c)
 
-        def quantise(planes, n, tag, late=False):
-            if late:
-                zq = ring.tile([P, n], U32, name="zq", tag="x01", bufs=XB, align_bytes=64)
-            else:
-                zq = keep.tile([P, n], U32, name="q" + tag, align_bytes=64)
+        def quantise(planes, n, tag):
+            zq = keep.tile([P, n], U32, name="q" + tag, align_bytes=64)
             zs = keep.tile([P, n], U8, name="s" + tag, align_bytes=64)
             nc.vector.quantize_mx(out=zq[:].bitcast(FP8X4), scales=zs[:], in_=planes[:].rearrange("p n t -> p (n t)"))
             return zq, zs
@@ -175,13 +184,12 @@ def tile_picked_irls8_none_po_kernel(
         window = [keep.tile([P, S], F32, name="window%d" % t) for t in range(4)]
         u_tags = (("b0", "b0", "b1", "b1"), ("b2", "b2", "b2", "b2"), ("b3", "a0", "a1", "a2"))
         upre = {}
-        rounded = {}
         sigs = {}
 
         def second_product(zb, c):
             lo, hi = CHUNKS1[c]
             n = hi - lo
-            zq, zs = quantise(zb, n, "z%d" % lo, c < last)
+            zq, zs = quantise(zb, n, "z%d" % lo)
             banks = {}
             for t in range(4):
                 tag = u_tags[c][t]
@@ -196,10 +204,7 @@ def tile_picked_irls8_none_po_kernel(
         def doubled(c):
             lo, hi = CHUNKS1[c]
             for t in (2, 3):
-                if c == last:
-                    nc.scalar.activation(out=window[t][:, lo:hi], in_=upre[c, t], func=ACT.Copy, scale=2.0)
-                else:
-                    nc.vector.tensor_scalar(out=window[t][:, lo:hi], in0=upre[c, t], scalar1=2.0, scalar2=None, op0=ALU.mult)
+                nc.scalar.activation(out=window[t][:, lo:hi], in_=upre[c, t], func=ACT.Identity, scale=2.0, bias=zero[:])
 
         def centre(dst, sig, t):
             nc.vector.tensor_scalar(out=dst, in0=sig, scalar1=0.5, scalar2=gain2[:, t : t + 1], op0=ALU.subtract, op1=ALU.mult)
@@ -208,8 +213,8 @@ def tile_picked_irls8_none_po_kernel(
             lo, hi = CHUNKS1[c]
             n = hi - lo
             if c < last:
-                sig = ring.tile([P, 2, n], F32, name="sig_early", tag="sq%d" % c, bufs=SQB)
-                nc.scalar.activation(out=sig[:].rearrange("p t n -> p (t n)"), in_=upre[c, "01"], func=ACT.Sigmoid, scale=2.0)
+                sig = keep.tile([P, 2, n], F32, name="sig_early%d" % c)
+                nc.scalar.activation(out=sig[:].rearrange("p t n -> p (t n)"), in_=upre[c, "01"], func=ACT.Sigmoid, scale=2.0, bias=zero[:])
             else:
                 sig = keep.tile([P, 2, n], F32, name="sig_last")
                 for t in (0, 1):
@@ -226,16 +231,17 @@ def tile_picked_irls8_none_po_kernel(
             n = hi - lo
             zt = keep.tile([P, n // P, 2, P, 2], BF16, name="zt%d" % c, align_bytes=64)
             for i in range(n // P):
-                nc.scalar.activation(out=zt[:, i], in_=sums[lo + i * P][:].rearrange("p (u e m) -> p u m e", u=2, e=2), func=ACT.Copy)
+                summed = sums[lo + i * P][:].rearrange("p (u e m) -> p u m e", u=2, e=2)
+                nc.scalar.activation(out=zt[:, i], in_=summed, func=ACT.Copy)
             words = zt[:].rearrange("p i u m e -> p (i u m e)").bitcast(F32)
             turned = psum.tile([P, 2 * n], F32, name="turned", tag="a%d" % (2 + c))
             for i in range(n // P):
                 for u in range(2):
                     nc.tensor.transpose(turned[:, u * n + i * P : u * n + (i + 1) * P], words[:, (2 * i + u) * P : (2 * i + u + 1) * P], ident[:])
             zb = keep.tile([P, n, 4], BF16, name="zb%d" % c, align_bytes=64)
-            nc.scalar.copy(out=zb[:].rearrange("p n t -> p (n t)").bitcast(F32).rearrange("p (n u) -> p n u", u=2),
-                           in_=turned[:].rearrange("p (u n) -> p n u", u=2))
-            rounded[c] = zb
+            pairs = zb[:].rearrange("p n t -> p (n t)").bitcast(F32).rearrange("p (n u) -> p n u", u=2)
+            nc.scalar.copy(out=pairs, in_=turned[:].rearrange("p (u n) -> p n u", u=2))
+            second_product(zb, c)
 
         part = keep.tile([P, 4, P], F32, name="part")
         z = keep.tile([P, 4, P], F32, name="z")
@@ -250,23 +256,23 @@ def tile_picked_irls8_none_po_kernel(
             front(c, t)
             if u >= LAG:
                 back(*units[u - LAG])
+        zero = ring.tile([P, 1], F32, name="zero", tag="sq1", bufs=SQB)
+        nc.gpsimd.memset(zero[:], 0.0)
         for c, t in units[-LAG:-1]:
             back(c, t)
         for c in range(last):
-            second_product(rounded[c], c)
             squash(c)
+            doubled(c)
         add_up(slice(0, 3))
         back(last, 3)
         add_third(slice(0, 3))
         add_up(slice(3, 4))
         add_third(slice(3, 4))
         zb_last = keep.tile([P, P, 4], BF16, name="zb_last", align_bytes=64)
-        nc.vector.tensor_copy(out=zb_last[:], in_=z[:].rearrange("p t n -> p n t"))
+        weave_vector(zb_last, z[:])
         second_product(zb_last, last)
         squash(last)
         doubled(last)
-        for c in range(last):
-            doubled(c)
         for c in range(last + 1):
             apply_gain(c)
 
@@ -289,7 +295,7 @@ def tile_picked_irls8_none_po_kernel(
             for t in (2, 3):
                 centre(g[:, t, :], sig[:, t - 2, :], t)
             zb = keep.tile([P, n, 4], BF16, name="z2b%d" % lo, align_bytes=64)
-            nc.scalar.activation(out=zb[:], in_=g[:].rearrange("p t n -> p n t"), func=ACT.Copy)
+            weave_scalar(zb, g[:])
             stage[c] = zb
 
         def last_product(c):
@@ -312,7 +318,10 @@ def tile_picked_irls8_none_po_kernel(
                 nc.vector.tensor_tensor(out=o[:, ts, :], in0=bank[:].rearrange("p (t n) -> p t n", n=n), in1=resid[:, ts, lo:hi], op=ALU.add)
             nc.sync.dma_start(out=out_rows[:, :, lo:hi], in_=o[:])
             ob = keep.tile([P, n, 4], BF16, name="ob%d" % lo, align_bytes=64)
-            nc.scalar.activation(out=ob[:], in_=o[:].rearrange("p t n -> p n t"), func=ACT.Copy)
+            if c == len(CHUNKS2) - 1:
+                weave_vector(ob, o[:])
+            else:
+                weave_scalar(ob, o[:])
             stage[c, "ob"] = ob
 
         def planes_out(c):

@@ -18,12 +18,14 @@ T = 2048
 S = 512
 FLOPS = 3 * 2 * 512 * 512 * 512
 
-CHUNKS1 = [(0, 256), (256, 384), (384, 512)]
-XB = 5
-GB = 4
-SQB = 1
+STRETCHES = [(0, 256), (256, 384), (384, 512)]
+TURNED_PLANES = (0,)
 LAG = 2
-CHUNKS2 = [(0, 128), (128, 256), (256, 384), (384, 512)]
+SLOTS = 44
+ROUND_AFTER = {0: 5, 1: 9}
+PAIR_AFTER = {0: 6, 1: 10}
+ADD_LAG = 2
+OUT_LAG = 3
 
 
 def tile_picked_irls8_none_po_kernel(
@@ -33,14 +35,20 @@ def tile_picked_irls8_none_po_kernel(
     nc = tc.nc
     with ExitStack() as ctx:
         keep = ctx.enter_context(tc.tile_pool(name="keep", bufs=1))
-        ring = ctx.enter_context(tc.tile_pool(name="ring", bufs=3))
+        ring = ctx.enter_context(tc.tile_pool(name="ring", bufs=SLOTS))
         psum = ctx.enter_context(tc.psum_pool(name="psum", bufs=1))
 
-        def words_view(w):
-            return w[0].rearrange("p n t -> p (n t)").bitcast(I32)
+        def work(shape, dtype):
+            return ring.tile(shape, dtype, name="work", tag="work", align_bytes=64)
 
-        def load_scales(plane, scales, row, quadrants):
-            for q in quadrants:
+        def bank(tag, shape=(P, S)):
+            return psum.tile(list(shape), F32, name="bank", tag=tag)
+
+        def words_view(words):
+            return words[0].rearrange("p n t -> p (n t)").bitcast(I32)
+
+        def load_scales(plane, scales, row):
+            for q in range(4):
                 nc.sync.dma_start(out=plane[32 * q + row : 32 * q + row + 4, :].bitcast(I32), in_=scales[0, 4 * q : 4 * q + 4, :].bitcast(I32))
 
         offs_t = keep.tile([P, S // 16], U16, name="offs_t")
@@ -49,13 +57,12 @@ def tile_picked_irls8_none_po_kernel(
         xs = keep.tile([P, T], U8, name="xs", align_bytes=64)
         w_raw = [keep.tile([P, S], I32, name="w_raw%d" % i, align_bytes=64) for i in range(3)]
         s_raw = [keep.tile([P, S], U8, name="s_raw%d" % i, align_bytes=64) for i in range(2)]
-        wq = [keep.tile([P, S], I32, name="wq%d" % i, align_bytes=64) for i in range(3)]
-        ws = [keep.tile([P, S], U8, name="ws%d" % i, align_bytes=64) for i in range(2)]
         gain = keep.tile([P, 4], F32, name="gain")
+        gain2 = keep.tile([P, 4], F32, name="gain2")
         resid = keep.tile([P, 4, S], F32, name="resid")
         warm = keep.tile([P, 2], F32, name="warm")
-
         ident = keep.tile([P, P], F32, name="ident")
+
         nc.vector.memset(xs[:].bitcast(I32), 0)
         nc.gpsimd.memset(s_raw[0][:].bitcast(I32), 0)
         nc.gpsimd.memset(warm[:, 0:1], 1.0)
@@ -65,282 +72,311 @@ def tile_picked_irls8_none_po_kernel(
 
         nc.sync.dma_start(offs_t[:], offs)
         nc.sync.dma_start(out=w_raw[0][:], in_=words_view(w1_words))
-        load_scales(xs, x_scales, 0, range(4))
+        load_scales(xs, x_scales, 0)
         nc.sync.dma_start(out=xw[:], in_=words_view(x_words))
-        load_scales(s_raw[0], w1_scales, 0, range(4))
-        for tile_, src in zip(lists[:3], (p1, p2, p3)):
-            nc.sync.dma_start(tile_[:], src)
-        nc.sync.dma_start(out=gain[:], in_=gn.rearrange("(p t) o -> p (t o)", t=4))
+        load_scales(s_raw[0], w1_scales, 0)
+        nc.sync.dma_start(lists[0][:], p1)
         nc.sync.dma_start(out=w_raw[1][:], in_=words_view(w2_words))
         nc.sync.dma_start(out=w_raw[2][:], in_=words_view(w3_words))
-        load_scales(s_raw[1], w2_scales, 0, range(4))
-        load_scales(s_raw[1], w3_scales, 4, range(4))
+        nc.sync.dma_start(lists[1][:], p2)
+        nc.sync.dma_start(lists[2][:], p3)
+        nc.sync.dma_start(out=gain[:], in_=gn.rearrange("(p t) o -> p (t o)", t=4))
+        load_scales(s_raw[1], w2_scales, 0)
+        load_scales(s_raw[1], w3_scales, 4)
         nc.sync.dma_start(lists[3][:], mv)
         nc.sync.dma_start(out=resid[:], in_=res.rearrange("(p t) s -> p t s", t=4))
 
-        def weave_views(dst, planes):
-            return dst[:].rearrange("p (c i) t -> p c t i", i=4), planes.rearrange("p t (c i) -> p c t i", i=4)
-
-        def weave_scalar(dst, planes):
-            out, in_ = weave_views(dst, planes)
-            nc.scalar.activation(out=out, in_=in_, func=ACT.Copy)
-
-        def weave_vector(dst, planes):
-            out, in_ = weave_views(dst, planes)
-            nc.vector.tensor_copy(out=out, in_=in_)
-
-        def deal(dst, src):
+        def deal(src, dst):
             nc.vector.tensor_copy(out=dst[:].rearrange("p (t m) -> p m t", t=4), in_=src[:].rearrange("p (m t) -> p m t", t=4))
+            return dst
 
-        def product(bank, i, t, codes, scales, lo, hi):
+        def product(out, w_codes, w_plane, row, t, codes, scales):
             m = slice(P * t, P * (t + 1))
-            plane = (ws[0][:, m], ws[1][:, m], ws[1][4:P, m])[i]
-            nc.tensor.matmul_mx(out=bank[:, lo:hi], lhsT=wq[i][:, m].bitcast(FP8X4), lhsT_scale=plane,
+            nc.tensor.matmul_mx(out=out, lhsT=w_codes[:, m].bitcast(FP8X4), lhsT_scale=w_plane[row:P, m],
                                 rhs=codes.bitcast(FP8X4), rhs_scale=scales, start=True, stop=True)
 
-        deal(wq[0], w_raw[0])
-        deal(ws[0], s_raw[0])
-        ybank = [psum.tile([P, S], F32, name="ybank%d" % t, tag="a%d" % t) for t in range(4)]
-        spare = psum.tile([P, S], F32, name="spare", tag="b0")
-        picked = []
-        ps = keep.tile([P, S], U8, name="ps", align_bytes=64)
-        nc.vector.tensor_copy(out=ps[:], in_=xs[:].indirect(offs_t[:]))
-        for lo, hi in ((0, 256), (256, 512)):
-            pw = keep.tile([P, hi - lo], U32, name="pw%d" % lo, align_bytes=64)
-            nc.vector.tensor_copy(out=pw[:], in_=xw[:].bitcast(U32).indirect(offs_t[:, lo // 16 : hi // 16]))
-            picked.append((pw, lo, hi))
+        def weave(engine, planes, n):
+            woven = work([P, n, 4], BF16)
+            out = woven[:].rearrange("p (c i) t -> p c t i", i=4)
+            in_ = planes.rearrange("p t (c i) -> p c t i", i=4)
+            if engine == "scalar":
+                nc.scalar.activation(out=out, in_=in_, func=ACT.Copy)
+            else:
+                nc.vector.tensor_copy(out=out, in_=in_)
+            return woven
+
+        def quantise(woven, n, name):
+            codes = work([P, n], U32)
+            scales = keep.tile([P, n], U8, name=name, align_bytes=64)
+            nc.vector.quantize_mx(out=codes[:].bitcast(FP8X4), scales=scales[:], in_=woven[:].rearrange("p n t -> p (n t)"))
+            return codes, scales
+
+        def pick_words(lo, hi):
+            picked = work([P, hi - lo], U32)
+            nc.vector.tensor_copy(out=picked[:], in_=xw[:].bitcast(U32).indirect(offs_t[:, lo // 16 : hi // 16]))
+            return picked
+
+        half = S // 2
+        w1_codes = deal(w_raw[0], work([P, S], I32))
+        picked_scales = work([P, S], U8)
+        nc.vector.tensor_copy(out=picked_scales[:], in_=xs[:].indirect(offs_t[:]))
+        picked = [pick_words(0, half)]
+        w1_plane = deal(s_raw[0], work([P, S], U8))
+        picked.append(pick_words(half, S))
+        w2_codes = deal(w_raw[1], keep.tile([P, S], I32, name="w2_codes", align_bytes=64))
+        w3_codes = deal(w_raw[2], keep.tile([P, S], I32, name="w3_codes", align_bytes=64))
         y = [keep.tile([P, S], F32, name="y%d" % t) for t in range(4)]
+        minus_y = {t: keep.tile([P, S], F32, name="minus_y%d" % t) for t in TURNED_PLANES}
         for t in range(4):
-            for i, (pw, lo, hi) in enumerate(picked):
-                bank = spare if (t, i) == (0, 1) else ybank[t]
-                product(bank, 0, t, pw[:], ps[:, lo:hi], lo, hi)
+            banks = [bank("a%d" % t)]
+            banks.append(bank("b0") if t == 0 else banks[0])
+            for i in range(2):
+                cols = slice(i * half, (i + 1) * half)
+                product(banks[i][:, cols], w1_codes, w1_plane, 0, t, picked[i][:], picked_scales[:, cols])
                 if t == 0:
-                    nc.scalar.copy(out=y[t][:, lo:hi], in_=bank[:, lo:hi])
+                    nc.scalar.copy(out=y[t][:, cols], in_=banks[i][:, cols])
             if t > 0:
-                nc.scalar.copy(out=y[t][:], in_=ybank[t][:])
-        deal(wq[1], w_raw[1])
-        deal(ws[1], s_raw[1])
-        deal(wq[2], w_raw[2])
+                nc.scalar.copy(out=y[t][:], in_=banks[0][:])
+            if t in TURNED_PLANES:
+                nc.scalar.activation(out=minus_y[t][:], in_=y[t][:], func=ACT.Copy, scale=-1.0)
+        nc.vector.tensor_scalar(out=gain2[:], in0=gain[:], scalar1=2.0, scalar2=None, op0=ALU.mult)
 
-        units = [(c, t) for c in range(len(CHUNKS1)) for t in range(4)]
-        last = len(CHUNKS1) - 1
-        r_last = keep.tile([P, 3, 4, P], F32, name="r_last")
-        sums = {}
-        xg = {}
-        wt = {}
+        units = [(c, t) for c in range(len(STRETCHES)) for t in range(4)]
+        last = len(STRETCHES) - 1
+        fetched, weights, terms, sums, rounded, woven_z, pre, sigs = {}, {}, {}, {}, {}, {}, {}, {}
 
-        def front(c, t):
-            lo, hi = CHUNKS1[c]
+        def fetch_neighbours(c, t):
+            lo, hi = STRETCHES[c]
             n = hi - lo
-            u = 4 * c + t
-            x = ring.tile([P, 3, n], F32, name="x", tag="xq", bufs=XB, align_bytes=64)
-            d = keep.tile([P, 3, n], F32, name="d%d" % u)
+            x = work([P, 3, n], F32)
             for k in range(3):
                 nc.vector.tensor_copy(out=x[:, k, :], in_=y[t][:].indirect(lists[k][:, lo // 16 : hi // 16]))
-            for k in range(3):
-                nc.gpsimd.tensor_tensor(out=d[:, k, :], in0=x[:, k, :], in1=y[t][:, lo:hi], op=ALU.subtract)
-            w = keep.tile([P, 3, n], F32, name="w%d" % u)
-            flat_d = d[:].rearrange("p k n -> p (k n)")
-            flat_w = w[:].rearrange("p k n -> p (k n)")
-            parts = (slice(0, 3 * n // 2), slice(3 * n // 2, 3 * n))
-            sq = [ring.tile([P, s.stop - s.start], F32, name="sq", tag="sq%d" % i, bufs=SQB) for i, s in enumerate(parts)]
-            for i, s in enumerate(parts):
-                nc.scalar.activation(out=sq[i][:], in_=flat_d[:, s], func=ACT.Square)
-            q = ring.tile([P, 3 * n], F32, name="q", tag="xq", bufs=XB, align_bytes=64)
-            for i, s in enumerate(parts):
-                nc.scalar.activation(out=q[:, s], in_=sq[i][:], func=ACT.Abs_reciprocal_sqrt, bias=1.0)
-            for s in parts:
-                nc.scalar.activation(out=flat_w[:, s], in_=q[:, s], func=ACT.Square)
-            xg[c, t] = x
-            wt[c, t] = w
-
-        def back(c, t):
-            lo, hi = CHUNKS1[c]
-            if c == last:
-                r = r_last[:, :, t, :]
+            fetched[c, t] = x
+            if t in TURNED_PLANES:
+                parts = []
+                for j in range(0, n, P):
+                    diff = bank("b%d" % (j // P), (P, 3 * P))
+                    for k in range(3):
+                        out = diff[:, k * P : (k + 1) * P]
+                        nc.tensor.matmul(out=out, lhsT=x[:, k, j : j + P], rhs=ident[:], start=True, stop=False, is_transpose=True)
+                        nc.tensor.matmul(out=out, lhsT=minus_y[t][:, lo + j : lo + j + P], rhs=ident[:], start=False, stop=True, is_transpose=True)
+                    parts.append(diff[:])
+                if len(parts) == 1:
+                    parts = [parts[0][:, : 3 * n // 2], parts[0][:, 3 * n // 2 :]]
             else:
-                r_tile = ring.tile([P, 3, hi - lo], F32, name="r", tag="r")
-                r = r_tile[:]
-            nc.vector.scalar_tensor_tensor(out=r, in0=xg[c, t][:], scalar=gain[:, t : t + 1], in1=wt[c, t][:], op0=ALU.mult, op1=ALU.mult)
+                d = work([P, 3, n], F32)
+                nc.vector.tensor_tensor(out=d[:, 0:2, :], in0=x[:, 0:2, :], in1=y[t][:, lo:hi].unsqueeze(1).to_broadcast([P, 2, n]), op=ALU.subtract)
+                nc.vector.tensor_tensor(out=d[:, 2, :], in0=x[:, 2, :], in1=y[t][:, lo:hi], op=ALU.subtract)
+                flat = d[:].rearrange("p k n -> p (k n)")
+                parts = [flat[:, : 3 * n // 2], flat[:, 3 * n // 2 :]]
+            return parts
+
+        def robust_weights(c, t, parts):
+            n = STRETCHES[c][1] - STRETCHES[c][0]
+            stages = []
+            for func, bias in ((ACT.Square, 0.0), (ACT.Abs_reciprocal_sqrt, 1.0), (ACT.Square, 0.0)):
+                result = work([P, 2, 3 * n // 2], F32)
+                for i in range(2):
+                    nc.scalar.activation(out=result[:, i, :], in_=parts[i], func=func, bias=bias)
+                parts = [result[:, 0, :], result[:, 1, :]]
+                stages.append(result)
+            w = stages[-1][:].rearrange("p i m -> p (i m)")
+            if t in TURNED_PLANES:
+                weights[c, t] = []
+                for j in range(n // P):
+                    turned_back = bank("b%d" % (2 + j), (P, 3, P))
+                    for k in range(3):
+                        nc.tensor.transpose(turned_back[:, k, :], w[:, (3 * j + k) * P : (3 * j + k + 1) * P], ident[:])
+                    weights[c, t].append(turned_back[:])
+            else:
+                weights[c, t] = [w.rearrange("p (k n) -> p k n", k=3)]
+
+        def weigh(c, t):
+            lo, hi = STRETCHES[c]
+            r = work([P, 3, hi - lo], F32)
+            terms[c, t] = r
+            width = (hi - lo) // len(weights[c, t])
+            for i, w in enumerate(weights[c, t]):
+                cols = slice(i * width, (i + 1) * width)
+                nc.vector.scalar_tensor_tensor(out=r[:, :, cols], in0=fetched[c, t][:, :, cols], scalar=gain[:, t : t + 1], in1=w,
+                                               op0=ALU.mult, op1=ALU.mult)
             if c == last:
                 return
             for j in range(lo, hi, P):
                 if t == 0:
-                    sums[j] = psum.tile([P, S], F32, name="sums", tag="a%d" % (j // P % 2))
+                    sums[j] = bank("a%d" % (j // P))
                 for k in range(3):
                     nc.tensor.matmul(out=sums[j][:, P * t : P * (t + 1)], lhsT=r[:, k, j - lo : j - lo + P], rhs=ident[:],
                                      start=(k == 0), stop=(k == 2), is_transpose=True)
-            if t == 3:
-                finish(c)
 
-        def quantise(planes, n, tag):
-            zq = keep.tile([P, n], U32, name="q" + tag, align_bytes=64)
-            zs = keep.tile([P, n], U8, name="s" + tag, align_bytes=64)
-            nc.vector.quantize_mx(out=zq[:].bitcast(FP8X4), scales=zs[:], in_=planes[:].rearrange("p n t -> p (n t)"))
-            return zq, zs
-
-        gain2 = keep.tile([P, 4], F32, name="gain2")
-        nc.vector.tensor_scalar(out=gain2[:], in0=gain[:], scalar1=2.0, scalar2=None, op0=ALU.mult)
-        window = [keep.tile([P, S], F32, name="window%d" % t) for t in range(4)]
-        u_tags = (("b0", "b0", "b1", "b1"), ("b2", "b2", "b2", "b2"), ("b3", "a0", "a1", "a2"))
-        upre = {}
-        sigs = {}
-
-        def second_product(zb, c):
-            lo, hi = CHUNKS1[c]
+        def round_sums(c):
+            lo, hi = STRETCHES[c]
             n = hi - lo
-            zq, zs = quantise(zb, n, "z%d" % lo)
+            zt = work([P, n // P, 2, P, 2], BF16)
+            for i in range(n // P):
+                nc.scalar.activation(out=zt[:, i], in_=sums[lo + i * P][:].rearrange("p (u e m) -> p u m e", u=2, e=2), func=ACT.Copy)
+            words = zt[:].rearrange("p i u m e -> p (i u m e)").bitcast(F32)
+            turned = bank("a3", (P, 2 * n))
+            for i in range(n // P):
+                for u in range(2):
+                    nc.tensor.transpose(turned[:, u * n + i * P : u * n + (i + 1) * P], words[:, (2 * i + u) * P : (2 * i + u + 1) * P], ident[:])
+            rounded[c] = turned
+
+        def pair_up(c):
+            n = STRETCHES[c][1] - STRETCHES[c][0]
+            woven = work([P, n, 4], BF16)
+            nc.scalar.copy(out=woven[:].rearrange("p n t -> p (n t)").bitcast(F32).rearrange("p (n u) -> p n u", u=2),
+                           in_=rounded[c][:].rearrange("p (u n) -> p n u", u=2))
+            woven_z[c] = woven
+
+        for u, (c, t) in enumerate(units):
+            parts = fetch_neighbours(c, t)
+            if u >= LAG:
+                weigh(*units[u - LAG])
+            robust_weights(c, t, parts)
+            for done in range(last):
+                if ROUND_AFTER[done] == u:
+                    round_sums(done)
+                if PAIR_AFTER[done] == u:
+                    pair_up(done)
+
+        table = work([P, 1], F32)
+        nc.scalar.activation(out=table[:], in_=warm[:, 0:1], func=ACT.Sigmoid)
+        window = {t: keep.tile([P, S], F32, name="window%d" % t) for t in (2, 3)}
+        u_tags = (("b0", "b0", "b1", "b1"), ("b2",) * 4, ("b3", "a0", "a1", "a2"))
+
+        def second_product(c):
+            n = STRETCHES[c][1] - STRETCHES[c][0]
+            codes, scales = quantise(woven_z[c], n, "z_scales%d" % c)
             banks = {}
             for t in range(4):
                 tag = u_tags[c][t]
                 place = u_tags[c][:t].count(tag) * n
                 if tag not in banks:
-                    banks[tag] = psum.tile([P, S], F32, name="ubank", tag=tag)
-                product(banks[tag], 1, t, zq[:], zs[:], place, place + n)
-                upre[c, t] = banks[tag][:, place : place + n]
-            if c < last:
-                upre[c, "01"] = banks[u_tags[c][0]][:, 0 : 2 * n]
-
-        def doubled(c):
-            lo, hi = CHUNKS1[c]
-            for t in (2, 3):
-                nc.scalar.activation(out=window[t][:, lo:hi], in_=upre[c, t], func=ACT.Identity, scale=2.0, bias=zero[:])
-
-        def centre(dst, sig, t):
-            nc.vector.tensor_scalar(out=dst, in0=sig, scalar1=0.5, scalar2=gain2[:, t : t + 1], op0=ALU.subtract, op1=ALU.mult)
+                    banks[tag] = bank(tag)
+                pre[c, t] = banks[tag][:, place : place + n]
+                product(pre[c, t], w2_codes, w23_plane, 0, t, codes[:], scales[:])
 
         def squash(c):
-            lo, hi = CHUNKS1[c]
-            n = hi - lo
-            if c < last:
-                sig = keep.tile([P, 2, n], F32, name="sig_early%d" % c)
-                nc.scalar.activation(out=sig[:].rearrange("p t n -> p (t n)"), in_=upre[c, "01"], func=ACT.Sigmoid, scale=2.0, bias=zero[:])
-            else:
-                sig = keep.tile([P, 2, n], F32, name="sig_last")
-                for t in (0, 1):
-                    nc.scalar.activation(out=sig[:, t, :], in_=upre[c, t], func=ACT.Sigmoid, scale=2.0)
+            lo, hi = STRETCHES[c]
+            sig = work([P, 2, hi - lo], F32)
+            for t in (0, 1):
+                nc.scalar.activation(out=sig[:, t, :], in_=pre[c, t], func=ACT.Sigmoid, scale=2.0)
+            for t in (2, 3):
+                nc.scalar.activation(out=window[t][:, lo:hi], in_=pre[c, t], func=ACT.Copy, scale=2.0)
             sigs[c] = sig
 
+        def centre(out, sig, t):
+            nc.vector.tensor_scalar(out=out, in0=sig, scalar1=0.5, scalar2=gain2[:, t : t + 1], op0=ALU.subtract, op1=ALU.mult)
+
         def apply_gain(c):
-            lo, hi = CHUNKS1[c]
+            lo, hi = STRETCHES[c]
             for t in (0, 1):
                 centre(window[t][:, lo:hi], sigs[c][:, t, :], t)
 
-        def finish(c):
-            lo, hi = CHUNKS1[c]
-            n = hi - lo
-            zt = keep.tile([P, n // P, 2, P, 2], BF16, name="zt%d" % c, align_bytes=64)
-            for i in range(n // P):
-                summed = sums[lo + i * P][:].rearrange("p (u e m) -> p u m e", u=2, e=2)
-                nc.scalar.activation(out=zt[:, i], in_=summed, func=ACT.Copy)
-            words = zt[:].rearrange("p i u m e -> p (i u m e)").bitcast(F32)
-            turned = psum.tile([P, 2 * n], F32, name="turned", tag="a%d" % (2 + c))
-            for i in range(n // P):
-                for u in range(2):
-                    nc.tensor.transpose(turned[:, u * n + i * P : u * n + (i + 1) * P], words[:, (2 * i + u) * P : (2 * i + u + 1) * P], ident[:])
-            zb = keep.tile([P, n, 4], BF16, name="zb%d" % c, align_bytes=64)
-            pairs = zb[:].rearrange("p n t -> p (n t)").bitcast(F32).rearrange("p (n u) -> p n u", u=2)
-            nc.scalar.copy(out=pairs, in_=turned[:].rearrange("p (u n) -> p n u", u=2))
-            second_product(zb, c)
+        z_last = keep.tile([P, 4, P], F32, name="z_last")
+        pairs = {}
 
-        part = keep.tile([P, 4, P], F32, name="part")
-        z = keep.tile([P, 4, P], F32, name="z")
+        def add_two(t):
+            pairs[t] = work([P, P], F32)
+            nc.vector.tensor_tensor(out=pairs[t][:], in0=terms[last, t][:, 0, :], in1=terms[last, t][:, 1, :], op=ALU.add)
 
-        def add_up(ts):
-            nc.vector.tensor_tensor(out=part[:, ts], in0=r_last[:, 0, ts], in1=r_last[:, 1, ts], op=ALU.add)
+        def add_third(t):
+            nc.vector.tensor_tensor(out=z_last[:, t, :], in0=pairs[t][:], in1=terms[last, t][:, 2, :], op=ALU.add)
 
-        def add_third(ts):
-            nc.vector.tensor_tensor(out=z[:, ts], in0=part[:, ts], in1=r_last[:, 2, ts], op=ALU.add)
-
-        for u, (c, t) in enumerate(units):
-            front(c, t)
-            if u >= LAG:
-                back(*units[u - LAG])
-        zero = ring.tile([P, 1], F32, name="zero", tag="sq1", bufs=SQB)
-        nc.gpsimd.memset(zero[:], 0.0)
-        for c, t in units[-LAG:-1]:
-            back(c, t)
-        for c in range(last):
-            squash(c)
-            doubled(c)
-        add_up(slice(0, 3))
-        back(last, 3)
-        add_third(slice(0, 3))
-        add_up(slice(3, 4))
-        add_third(slice(3, 4))
-        zb_last = keep.tile([P, P, 4], BF16, name="zb_last", align_bytes=64)
-        weave_vector(zb_last, z[:])
-        second_product(zb_last, last)
+        add_two(0)
+        add_two(1)
+        w23_plane = deal(s_raw[1], work([P, S], U8))
+        add_third(0)
+        add_third(1)
+        second_product(0)
+        squash(0)
+        weigh(last, 2)
+        weigh(last, 3)
+        add_two(2)
+        add_two(3)
+        add_third(2)
+        second_product(1)
+        squash(1)
+        add_third(3)
+        woven_z[last] = weave("vector", z_last[:], P)
+        second_product(last)
         squash(last)
-        doubled(last)
+        for t in (0, 1):
+            window[t] = work([P, S], F32)
         for c in range(last + 1):
             apply_gain(c)
 
-        oq = keep.tile([P, S], U32, name="oq", align_bytes=64)
-        osc = keep.tile([P, S], U8, name="osc", align_bytes=64)
+        out_scales = keep.tile([P, S], U8, name="out_scales", align_bytes=64)
         out_rows = out_0.rearrange("(p t) s -> p t s", t=4)
         out_words = words_view(out_1)
-        stage = {}
+        pieces = S // P
+        moved_sigs, moved, woven_z2, products, results, woven_out = {}, {}, {}, {}, {}, {}
 
-        def fetch(c):
-            lo, hi = CHUNKS2[c]
-            n = hi - lo
-            g = ring.tile([P, 4, n], BF16, name="g", tag="g", bufs=GB, align_bytes=64)
-            entries = lists[3][:, lo // 16 : hi // 16]
-            sig = ring.tile([P, 2, n], F32, name="sig", tag="sig", bufs=2)
+        def entries_of(c):
+            return lists[3][:, c * P // 16 : (c + 1) * P // 16]
+
+        def fetch_squashed(c):
+            entries = entries_of(c)
+            sig = work([P, 2, P], F32)
             for t in (2, 3):
                 nc.scalar.activation(out=sig[:, t - 2, :], in_=window[t][:].indirect(entries), func=ACT.Sigmoid)
+            moved_sigs[c] = sig
+
+        def fetch_moved(c):
+            entries = entries_of(c)
+            sig = moved_sigs[c]
+            z2 = work([P, 4, P], BF16)
             for t in (0, 1):
-                nc.vector.tensor_copy(out=g[:, t, :], in_=window[t][:].indirect(entries))
+                nc.vector.tensor_copy(out=z2[:, t, :], in_=window[t][:].indirect(entries))
             for t in (2, 3):
-                centre(g[:, t, :], sig[:, t - 2, :], t)
-            zb = keep.tile([P, n, 4], BF16, name="z2b%d" % lo, align_bytes=64)
-            weave_scalar(zb, g[:])
-            stage[c] = zb
+                centre(z2[:, t, :], sig[:, t - 2, :], t)
+            moved[c] = z2
+
+        def weave_moved(c):
+            woven_z2[c] = weave("scalar", moved[c][:], P)
 
         def last_product(c):
-            lo, hi = CHUNKS2[c]
-            n = hi - lo
-            zq, zs = quantise(stage[c], n, "z2%d" % lo)
-            per_bank = S // n
-            banks = [psum.tile([P, S], F32, name="obank", tag="b%d" % c) for b in range(4 // per_bank)]
+            codes, scales = quantise(woven_z2[c], P, "z2_scales%d" % c)
+            products[c] = bank("b%d" % c)
             for t in range(4):
-                product(banks[t // per_bank], 2, t, zq[:], zs[:], (t % per_bank) * n, (t % per_bank + 1) * n)
-            stage[c] = banks
+                product(products[c][:, P * t : P * (t + 1)], w3_codes, w23_plane, 4, t, codes[:], scales[:])
 
-        def way_out(c):
-            lo, hi = CHUNKS2[c]
-            n = hi - lo
-            per_bank = S // n
-            o = keep.tile([P, 4, n], F32, name="o%d" % lo)
-            for b, bank in enumerate(stage[c]):
-                ts = slice(b * per_bank, (b + 1) * per_bank)
-                nc.vector.tensor_tensor(out=o[:, ts, :], in0=bank[:].rearrange("p (t n) -> p t n", n=n), in1=resid[:, ts, lo:hi], op=ALU.add)
-            nc.sync.dma_start(out=out_rows[:, :, lo:hi], in_=o[:])
-            ob = keep.tile([P, n, 4], BF16, name="ob%d" % lo, align_bytes=64)
-            if c == len(CHUNKS2) - 1:
-                weave_vector(ob, o[:])
-            else:
-                weave_scalar(ob, o[:])
-            stage[c, "ob"] = ob
+        def add_residual(c):
+            cols = slice(c * P, (c + 1) * P)
+            result = work([P, 4, P], F32)
+            nc.vector.tensor_tensor(out=result[:], in0=products[c][:].rearrange("p (t n) -> p t n", t=4), in1=resid[:, :, cols], op=ALU.add)
+            nc.sync.dma_start(out=out_rows[:, :, cols], in_=result[:])
+            results[c] = result
+
+        def weave_out(c):
+            woven_out[c] = weave("vector" if c == pieces - 1 else "scalar", results[c][:], P)
 
         def planes_out(c):
-            lo, hi = CHUNKS2[c]
-            nc.vector.quantize_mx(out=oq[:, lo:hi].bitcast(FP8X4), scales=osc[:, lo:hi], in_=stage[c, "ob"][:].rearrange("p n t -> p (n t)"))
-            if hi >= 384:
-                first = 0 if hi == 384 else lo
-                nc.sync.dma_start(out=out_words[:, first:hi], in_=oq[:, first:hi].bitcast(I32))
+            cols = slice(c * P, (c + 1) * P)
+            nc.vector.quantize_mx(out=out_codes[:, cols].bitcast(FP8X4), scales=out_scales[:, cols], in_=woven_out[c][:].rearrange("p n t -> p (n t)"))
+            if c % 2:
+                both = slice((c - 1) * P, (c + 1) * P)
+                nc.sync.dma_start(out=out_words[:, both], in_=out_codes[:, both].bitcast(I32))
 
-        for c in range(len(CHUNKS2)):
-            fetch(c)
+        fetch_squashed(0)
+        for c in range(pieces):
+            fetch_moved(c)
             if c > 0:
                 last_product(c - 1)
-        last_product(len(CHUNKS2) - 1)
-        for c in range(len(CHUNKS2)):
-            way_out(c)
-            if c > 0:
-                planes_out(c - 1)
-        planes_out(len(CHUNKS2) - 1)
+            if c + 1 < pieces:
+                fetch_squashed(c + 1)
+            weave_moved(c)
+        add_residual(0)
+        last_product(pieces - 1)
+        for c in range(1, pieces):
+            add_residual(c)
+            weave_out(c - 1)
+        out_codes = work([P, S], U32)
+        planes_out(0)
+        weave_out(pieces - 1)
+        for c in range(1, pieces):
+            planes_out(c)
         for q in range(4):
             queue = nc.scalar if q % 2 else nc.sync
-            queue.dma_start(out=out_2[0, 4 * q : 4 * q + 4, :].bitcast(I32), in_=osc[32 * q : 32 * q + 4, :].bitcast(I32))
+            queue.dma_start(out=out_2[0, 4 * q : 4 * q + 4, :].bitcast(I32), in_=out_scales[32 * q : 32 * q + 4, :].bitcast(I32))

@@ -16,16 +16,17 @@ ALU = mybir.AluOpType
 P = 128
 T = 2048
 S = 512
+PLANES = 4
+TERMS = 3
+PER_COLUMN = 16
 FLOPS = 3 * 2 * 512 * 512 * 512
 
-STRETCHES = [(0, 256), (256, 384), (384, 512)]
-TURNED_PLANES = (0,)
+STRETCHES = ((0, 256), (256, 384), (384, 512))
+TURNED_PLANE = 0
+VECTOR_PLANES = (0, 1)
+SCALAR_PLANES = (2, 3)
 LAG = 2
 SLOTS = 44
-ROUND_AFTER = {0: 5, 1: 9}
-PAIR_AFTER = {0: 6, 1: 10}
-ADD_LAG = 2
-OUT_LAG = 3
 
 
 def tile_picked_irls8_none_po_kernel(
@@ -47,56 +48,62 @@ def tile_picked_irls8_none_po_kernel(
         def words_view(words):
             return words[0].rearrange("p n t -> p (n t)").bitcast(I32)
 
-        def load_scales(plane, scales, row):
+        def load_scales(tile, scales, row):
             for q in range(4):
-                nc.sync.dma_start(out=plane[32 * q + row : 32 * q + row + 4, :].bitcast(I32), in_=scales[0, 4 * q : 4 * q + 4, :].bitcast(I32))
+                nc.sync.dma_start(out=tile[32 * q + row : 32 * q + row + 4, :].bitcast(I32), in_=scales[0, 4 * q : 4 * q + 4, :].bitcast(I32))
 
-        offs_t = keep.tile([P, S // 16], U16, name="offs_t")
-        lists = [keep.tile([P, S // 16], U16, name="list%d" % i) for i in range(4)]
-        xw = keep.tile([P, T], I32, name="xw", align_bytes=64)
-        xs = keep.tile([P, T], U8, name="xs", align_bytes=64)
-        w_raw = [keep.tile([P, S], I32, name="w_raw%d" % i, align_bytes=64) for i in range(3)]
-        s_raw = [keep.tile([P, S], U8, name="s_raw%d" % i, align_bytes=64) for i in range(2)]
-        gain = keep.tile([P, 4], F32, name="gain")
-        gain2 = keep.tile([P, 4], F32, name="gain2")
-        resid = keep.tile([P, 4, S], F32, name="resid")
+        def entries(held, lo, hi):
+            return held[:, lo // PER_COLUMN : hi // PER_COLUMN]
+
+        picks = keep.tile([P, S // PER_COLUMN], U16, name="picks")
+        neighbours = [keep.tile([P, S // PER_COLUMN], U16, name="neighbours%d" % k) for k in range(TERMS)]
+        moves = keep.tile([P, S // PER_COLUMN], U16, name="moves")
+        table_words = keep.tile([P, T], I32, name="table_words", align_bytes=64)
+        table_scales = keep.tile([P, T], U8, name="table_scales", align_bytes=64)
+        raw_words = [keep.tile([P, S], I32, name="raw_words%d" % i, align_bytes=64) for i in range(3)]
+        raw_scales_1 = keep.tile([P, S], U8, name="raw_scales_1", align_bytes=64)
+        raw_scales_23 = keep.tile([P, S], U8, name="raw_scales_23", align_bytes=64)
+        w3_row = 4
+        gain = keep.tile([P, PLANES], F32, name="gain")
+        twice_gain = keep.tile([P, PLANES], F32, name="twice_gain")
+        residual = keep.tile([P, PLANES, S], F32, name="residual")
         warm = keep.tile([P, 2], F32, name="warm")
-        ident = keep.tile([P, P], F32, name="ident")
+        identity = keep.tile([P, P], F32, name="identity")
 
-        nc.vector.memset(xs[:].bitcast(I32), 0)
-        nc.gpsimd.memset(s_raw[0][:].bitcast(I32), 0)
+        nc.vector.memset(table_scales[:].bitcast(I32), 0)
+        nc.gpsimd.memset(raw_scales_1[:].bitcast(I32), 0)
         nc.gpsimd.memset(warm[:, 0:1], 1.0)
         nc.scalar.activation(out=warm[:, 1:2], in_=warm[:, 0:1], func=ACT.Abs_reciprocal_sqrt)
-        nc.gpsimd.memset(s_raw[1][:].bitcast(I32), 0)
-        make_identity(nc, ident[:])
+        nc.gpsimd.memset(raw_scales_23[:].bitcast(I32), 0)
+        make_identity(nc, identity[:])
 
-        nc.sync.dma_start(offs_t[:], offs)
-        nc.sync.dma_start(out=w_raw[0][:], in_=words_view(w1_words))
-        load_scales(xs, x_scales, 0)
-        nc.sync.dma_start(out=xw[:], in_=words_view(x_words))
-        load_scales(s_raw[0], w1_scales, 0)
-        nc.sync.dma_start(lists[0][:], p1)
-        nc.sync.dma_start(out=w_raw[1][:], in_=words_view(w2_words))
-        nc.sync.dma_start(out=w_raw[2][:], in_=words_view(w3_words))
-        nc.sync.dma_start(lists[1][:], p2)
-        nc.sync.dma_start(lists[2][:], p3)
-        nc.sync.dma_start(out=gain[:], in_=gn.rearrange("(p t) o -> p (t o)", t=4))
-        load_scales(s_raw[1], w2_scales, 0)
-        load_scales(s_raw[1], w3_scales, 4)
-        nc.sync.dma_start(lists[3][:], mv)
-        nc.sync.dma_start(out=resid[:], in_=res.rearrange("(p t) s -> p t s", t=4))
+        nc.sync.dma_start(picks[:], offs)
+        nc.sync.dma_start(out=raw_words[0][:], in_=words_view(w1_words))
+        load_scales(table_scales, x_scales, 0)
+        nc.sync.dma_start(out=table_words[:], in_=words_view(x_words))
+        load_scales(raw_scales_1, w1_scales, 0)
+        nc.sync.dma_start(neighbours[0][:], p1)
+        nc.sync.dma_start(out=raw_words[1][:], in_=words_view(w2_words))
+        nc.sync.dma_start(out=raw_words[2][:], in_=words_view(w3_words))
+        nc.sync.dma_start(neighbours[1][:], p2)
+        nc.sync.dma_start(neighbours[2][:], p3)
+        nc.sync.dma_start(out=gain[:], in_=gn.rearrange("(p t) o -> p (t o)", t=PLANES))
+        load_scales(raw_scales_23, w2_scales, 0)
+        load_scales(raw_scales_23, w3_scales, w3_row)
+        nc.sync.dma_start(moves[:], mv)
+        nc.sync.dma_start(out=residual[:], in_=res.rearrange("(p t) s -> p t s", t=PLANES))
 
-        def deal(src, dst):
-            nc.vector.tensor_copy(out=dst[:].rearrange("p (t m) -> p m t", t=4), in_=src[:].rearrange("p (m t) -> p m t", t=4))
-            return dst
+        def deal(raw, dealt):
+            nc.vector.tensor_copy(out=dealt[:].rearrange("p (t m) -> p m t", t=PLANES), in_=raw[:].rearrange("p (m t) -> p m t", t=PLANES))
+            return dealt
 
-        def product(out, w_codes, w_plane, row, t, codes, scales):
+        def product(out, w_codes, w_scales, row, t, codes, scales):
             m = slice(P * t, P * (t + 1))
-            nc.tensor.matmul_mx(out=out, lhsT=w_codes[:, m].bitcast(FP8X4), lhsT_scale=w_plane[row:P, m],
+            nc.tensor.matmul_mx(out=out, lhsT=w_codes[:, m].bitcast(FP8X4), lhsT_scale=w_scales[row:P, m],
                                 rhs=codes.bitcast(FP8X4), rhs_scale=scales, start=True, stop=True)
 
-        def weave(engine, planes, n):
-            woven = work([P, n, 4], BF16)
+        def weave(engine, planes):
+            woven = work([P, P, PLANES], BF16)
             out = woven[:].rearrange("p (c i) t -> p c t i", i=4)
             in_ = planes.rearrange("p t (c i) -> p c t i", i=4)
             if engine == "scalar":
@@ -112,88 +119,86 @@ def tile_picked_irls8_none_po_kernel(
             return codes, scales
 
         def pick_words(lo, hi):
-            picked = work([P, hi - lo], U32)
-            nc.vector.tensor_copy(out=picked[:], in_=xw[:].bitcast(U32).indirect(offs_t[:, lo // 16 : hi // 16]))
-            return picked
+            words = work([P, hi - lo], U32)
+            nc.vector.tensor_copy(out=words[:], in_=table_words[:].bitcast(U32).indirect(entries(picks, lo, hi)))
+            return words
 
         half = S // 2
-        w1_codes = deal(w_raw[0], work([P, S], I32))
+        w1_codes = deal(raw_words[0], work([P, S], I32))
         picked_scales = work([P, S], U8)
-        nc.vector.tensor_copy(out=picked_scales[:], in_=xs[:].indirect(offs_t[:]))
+        nc.vector.tensor_copy(out=picked_scales[:], in_=table_scales[:].indirect(picks[:]))
         picked = [pick_words(0, half)]
-        w1_plane = deal(s_raw[0], work([P, S], U8))
+        w1_dealt_scales = deal(raw_scales_1, work([P, S], U8))
         picked.append(pick_words(half, S))
-        w2_codes = deal(w_raw[1], keep.tile([P, S], I32, name="w2_codes", align_bytes=64))
-        w3_codes = deal(w_raw[2], keep.tile([P, S], I32, name="w3_codes", align_bytes=64))
-        y = [keep.tile([P, S], F32, name="y%d" % t) for t in range(4)]
-        minus_y = {t: keep.tile([P, S], F32, name="minus_y%d" % t) for t in TURNED_PLANES}
-        for t in range(4):
+        w2_codes = deal(raw_words[1], keep.tile([P, S], I32, name="w2_codes", align_bytes=64))
+        w3_codes = deal(raw_words[2], keep.tile([P, S], I32, name="w3_codes", align_bytes=64))
+        y = [keep.tile([P, S], F32, name="y%d" % t) for t in range(PLANES)]
+        minus_y = keep.tile([P, S], F32, name="minus_y")
+        for t in range(PLANES):
             banks = [bank("a%d" % t)]
             banks.append(bank("b0") if t == 0 else banks[0])
             for i in range(2):
                 cols = slice(i * half, (i + 1) * half)
-                product(banks[i][:, cols], w1_codes, w1_plane, 0, t, picked[i][:], picked_scales[:, cols])
+                product(banks[i][:, cols], w1_codes, w1_dealt_scales, 0, t, picked[i][:], picked_scales[:, cols])
                 if t == 0:
                     nc.scalar.copy(out=y[t][:, cols], in_=banks[i][:, cols])
             if t > 0:
                 nc.scalar.copy(out=y[t][:], in_=banks[0][:])
-            if t in TURNED_PLANES:
-                nc.scalar.activation(out=minus_y[t][:], in_=y[t][:], func=ACT.Copy, scale=-1.0)
-        nc.vector.tensor_scalar(out=gain2[:], in0=gain[:], scalar1=2.0, scalar2=None, op0=ALU.mult)
+            if t == TURNED_PLANE:
+                nc.scalar.activation(out=minus_y[:], in_=y[t][:], func=ACT.Copy, scale=-1.0)
+        nc.vector.tensor_scalar(out=twice_gain[:], in0=gain[:], scalar1=2.0, scalar2=None, op0=ALU.mult)
 
-        units = [(c, t) for c in range(len(STRETCHES)) for t in range(4)]
+        units = [(c, t) for c in range(len(STRETCHES)) for t in range(PLANES)]
         last = len(STRETCHES) - 1
-        fetched, weights, terms, sums, rounded, woven_z, pre, sigs = {}, {}, {}, {}, {}, {}, {}, {}
+        fetched, weights, terms, sums, word_pairs, woven_z = {}, {}, {}, {}, {}, {}
 
-        def fetch_neighbours(c, t):
+        def in_halves(flat):
+            middle = flat.shape[1] // 2
+            return [flat[:, :middle], flat[:, middle:]]
+
+        def differences(c, t):
             lo, hi = STRETCHES[c]
             n = hi - lo
-            x = work([P, 3, n], F32)
-            for k in range(3):
-                nc.vector.tensor_copy(out=x[:, k, :], in_=y[t][:].indirect(lists[k][:, lo // 16 : hi // 16]))
+            x = work([P, TERMS, n], F32)
+            for k in range(TERMS):
+                nc.vector.tensor_copy(out=x[:, k, :], in_=y[t][:].indirect(entries(neighbours[k], lo, hi)))
             fetched[c, t] = x
-            if t in TURNED_PLANES:
-                parts = []
-                for j in range(0, n, P):
-                    diff = bank("b%d" % (j // P), (P, 3 * P))
-                    for k in range(3):
-                        out = diff[:, k * P : (k + 1) * P]
-                        nc.tensor.matmul(out=out, lhsT=x[:, k, j : j + P], rhs=ident[:], start=True, stop=False, is_transpose=True)
-                        nc.tensor.matmul(out=out, lhsT=minus_y[t][:, lo + j : lo + j + P], rhs=ident[:], start=False, stop=True, is_transpose=True)
-                    parts.append(diff[:])
-                if len(parts) == 1:
-                    parts = [parts[0][:, : 3 * n // 2], parts[0][:, 3 * n // 2 :]]
-            else:
-                d = work([P, 3, n], F32)
-                nc.vector.tensor_tensor(out=d[:, 0:2, :], in0=x[:, 0:2, :], in1=y[t][:, lo:hi].unsqueeze(1).to_broadcast([P, 2, n]), op=ALU.subtract)
-                nc.vector.tensor_tensor(out=d[:, 2, :], in0=x[:, 2, :], in1=y[t][:, lo:hi], op=ALU.subtract)
-                flat = d[:].rearrange("p k n -> p (k n)")
-                parts = [flat[:, : 3 * n // 2], flat[:, 3 * n // 2 :]]
-            return parts
+            if t == TURNED_PLANE:
+                turned = [bank("b%d" % i, (P, TERMS * P)) for i in range(n // P)]
+                for k in range(TERMS):
+                    for i, diff in enumerate(turned):
+                        nc.tensor.matmul(out=diff[:, k * P : (k + 1) * P], lhsT=minus_y[:, lo + i * P : lo + (i + 1) * P], rhs=identity[:],
+                                         start=True, stop=False, is_transpose=True)
+                    for i, diff in enumerate(turned):
+                        nc.tensor.matmul(out=diff[:, k * P : (k + 1) * P], lhsT=x[:, k, i * P : (i + 1) * P], rhs=identity[:],
+                                         start=False, stop=True, is_transpose=True)
+                return [diff[:] for diff in turned] if n > P else in_halves(turned[0][:])
+            d = work([P, TERMS, n], F32)
+            nc.vector.tensor_tensor(out=d[:, 0:2, :], in0=x[:, 0:2, :], in1=y[t][:, lo:hi].unsqueeze(1).to_broadcast([P, 2, n]), op=ALU.subtract)
+            nc.vector.tensor_tensor(out=d[:, 2, :], in0=x[:, 2, :], in1=y[t][:, lo:hi], op=ALU.subtract)
+            return in_halves(d[:].rearrange("p k n -> p (k n)"))
 
         def robust_weights(c, t, parts):
             n = STRETCHES[c][1] - STRETCHES[c][0]
-            stages = []
             for func, bias in ((ACT.Square, 0.0), (ACT.Abs_reciprocal_sqrt, 1.0), (ACT.Square, 0.0)):
-                result = work([P, 2, 3 * n // 2], F32)
+                stage = work([P, 2, TERMS * n // 2], F32)
                 for i in range(2):
-                    nc.scalar.activation(out=result[:, i, :], in_=parts[i], func=func, bias=bias)
-                parts = [result[:, 0, :], result[:, 1, :]]
-                stages.append(result)
-            w = stages[-1][:].rearrange("p i m -> p (i m)")
-            if t in TURNED_PLANES:
+                    nc.scalar.activation(out=stage[:, i, :], in_=parts[i], func=func, bias=bias)
+                parts = [stage[:, 0, :], stage[:, 1, :]]
+            w = stage[:].rearrange("p i m -> p (i m)")
+            if t == TURNED_PLANE:
                 weights[c, t] = []
-                for j in range(n // P):
-                    turned_back = bank("b%d" % (2 + j), (P, 3, P))
-                    for k in range(3):
-                        nc.tensor.transpose(turned_back[:, k, :], w[:, (3 * j + k) * P : (3 * j + k + 1) * P], ident[:])
+                for i in range(n // P):
+                    turned_back = bank("b%d" % (2 + i), (P, TERMS, P))
+                    for k in range(TERMS):
+                        nc.tensor.transpose(turned_back[:, k, :], w[:, (TERMS * i + k) * P : (TERMS * i + k + 1) * P], identity[:])
                     weights[c, t].append(turned_back[:])
             else:
-                weights[c, t] = [w.rearrange("p (k n) -> p k n", k=3)]
+                weights[c, t] = [w.rearrange("p (k n) -> p k n", k=TERMS)]
 
         def weigh(c, t):
             lo, hi = STRETCHES[c]
-            r = work([P, 3, hi - lo], F32)
+            r = work([P, TERMS, hi - lo], F32)
             terms[c, t] = r
             width = (hi - lo) // len(weights[c, t])
             for i, w in enumerate(weights[c, t]):
@@ -205,88 +210,96 @@ def tile_picked_irls8_none_po_kernel(
             for j in range(lo, hi, P):
                 if t == 0:
                     sums[j] = bank("a%d" % (j // P))
-                for k in range(3):
-                    nc.tensor.matmul(out=sums[j][:, P * t : P * (t + 1)], lhsT=r[:, k, j - lo : j - lo + P], rhs=ident[:],
-                                     start=(k == 0), stop=(k == 2), is_transpose=True)
+                for k in range(TERMS):
+                    nc.tensor.matmul(out=sums[j][:, P * t : P * (t + 1)], lhsT=r[:, k, j - lo : j - lo + P], rhs=identity[:],
+                                     start=(k == 0), stop=(k == TERMS - 1), is_transpose=True)
 
         def round_sums(c):
             lo, hi = STRETCHES[c]
             n = hi - lo
-            zt = work([P, n // P, 2, P, 2], BF16)
+            rounded = work([P, n // P, 2, P, 2], BF16)
             for i in range(n // P):
-                nc.scalar.activation(out=zt[:, i], in_=sums[lo + i * P][:].rearrange("p (u e m) -> p u m e", u=2, e=2), func=ACT.Copy)
-            words = zt[:].rearrange("p i u m e -> p (i u m e)").bitcast(F32)
-            turned = bank("a3", (P, 2 * n))
+                nc.scalar.activation(out=rounded[:, i], in_=sums[lo + i * P][:].rearrange("p (u e m) -> p u m e", u=2, e=2), func=ACT.Copy)
+            as_words = rounded[:].rearrange("p i u m e -> p (i u m e)").bitcast(F32)
+            word_pairs[c] = bank("a3", (P, 2 * n))
             for i in range(n // P):
                 for u in range(2):
-                    nc.tensor.transpose(turned[:, u * n + i * P : u * n + (i + 1) * P], words[:, (2 * i + u) * P : (2 * i + u + 1) * P], ident[:])
-            rounded[c] = turned
+                    nc.tensor.transpose(word_pairs[c][:, u * n + i * P : u * n + (i + 1) * P],
+                                        as_words[:, (2 * i + u) * P : (2 * i + u + 1) * P], identity[:])
 
-        def pair_up(c):
+        def join_pairs(c):
             n = STRETCHES[c][1] - STRETCHES[c][0]
-            woven = work([P, n, 4], BF16)
-            nc.scalar.copy(out=woven[:].rearrange("p n t -> p (n t)").bitcast(F32).rearrange("p (n u) -> p n u", u=2),
-                           in_=rounded[c][:].rearrange("p (u n) -> p n u", u=2))
-            woven_z[c] = woven
+            woven_z[c] = work([P, n, PLANES], BF16)
+            nc.scalar.copy(out=woven_z[c][:].rearrange("p n t -> p (n t)").bitcast(F32).rearrange("p (n u) -> p n u", u=2),
+                           in_=word_pairs[c][:].rearrange("p (u n) -> p n u", u=2))
 
-        for u, (c, t) in enumerate(units):
-            parts = fetch_neighbours(c, t)
-            if u >= LAG:
-                weigh(*units[u - LAG])
+        for step, (c, t) in enumerate(units):
+            parts = differences(c, t)
+            if step >= LAG:
+                weigh(*units[step - LAG])
             robust_weights(c, t, parts)
             for done in range(last):
-                if ROUND_AFTER[done] == u:
+                weighed_at = PLANES * done + PLANES - 1 + LAG
+                if step == weighed_at:
                     round_sums(done)
-                if PAIR_AFTER[done] == u:
-                    pair_up(done)
+                if step == weighed_at + 1:
+                    join_pairs(done)
 
-        table = work([P, 1], F32)
-        nc.scalar.activation(out=table[:], in_=warm[:, 0:1], func=ACT.Sigmoid)
-        window = {t: keep.tile([P, S], F32, name="window%d" % t) for t in (2, 3)}
-        u_tags = (("b0", "b0", "b1", "b1"), ("b2",) * 4, ("b3", "a0", "a1", "a2"))
+        warm_sigmoid = work([P, 1], F32)
+        nc.scalar.activation(out=warm_sigmoid[:], in_=warm[:, 0:1], func=ACT.Sigmoid)
+
+        u_banks = (("b0", "b0", "b1", "b1"), ("b2",) * PLANES, ("b3", "a0", "a1", "a2"))
+        u_planes, u_first_two, squashed, window = {}, {}, {}, {}
 
         def second_product(c):
             n = STRETCHES[c][1] - STRETCHES[c][0]
             codes, scales = quantise(woven_z[c], n, "z_scales%d" % c)
             banks = {}
-            for t in range(4):
-                tag = u_tags[c][t]
-                place = u_tags[c][:t].count(tag) * n
+            for t in range(PLANES):
+                tag = u_banks[c][t]
+                place = u_banks[c][:t].count(tag) * n
                 if tag not in banks:
                     banks[tag] = bank(tag)
-                pre[c, t] = banks[tag][:, place : place + n]
-                product(pre[c, t], w2_codes, w23_plane, 0, t, codes[:], scales[:])
+                u_planes[c, t] = banks[tag][:, place : place + n]
+                product(u_planes[c, t], w2_codes, w23_dealt_scales, 0, t, codes[:], scales[:])
+            if c < last:
+                u_first_two[c] = banks[u_banks[c][0]][:, 0 : 2 * n]
 
         def squash(c):
             lo, hi = STRETCHES[c]
-            sig = work([P, 2, hi - lo], F32)
-            for t in (0, 1):
-                nc.scalar.activation(out=sig[:, t, :], in_=pre[c, t], func=ACT.Sigmoid, scale=2.0)
-            for t in (2, 3):
-                nc.scalar.activation(out=window[t][:, lo:hi], in_=pre[c, t], func=ACT.Copy, scale=2.0)
-            sigs[c] = sig
-
-        def centre(out, sig, t):
-            nc.vector.tensor_scalar(out=out, in0=sig, scalar1=0.5, scalar2=gain2[:, t : t + 1], op0=ALU.subtract, op1=ALU.mult)
+            squashed[c] = work([P, len(VECTOR_PLANES), hi - lo], F32)
+            if c < last:
+                nc.scalar.activation(out=squashed[c][:].rearrange("p t n -> p (t n)"), in_=u_first_two[c], func=ACT.Tanh)
+            else:
+                for t in VECTOR_PLANES:
+                    nc.scalar.activation(out=squashed[c][:, t, :], in_=u_planes[c, t], func=ACT.Tanh)
 
         def apply_gain(c):
             lo, hi = STRETCHES[c]
-            for t in (0, 1):
-                centre(window[t][:, lo:hi], sigs[c][:, t, :], t)
+            for t in VECTOR_PLANES:
+                nc.vector.tensor_scalar(out=window[t][:, lo:hi], in0=squashed[c][:, t, :], scalar1=gain[:, t : t + 1], scalar2=None, op0=ALU.mult)
 
-        z_last = keep.tile([P, 4, P], F32, name="z_last")
-        pairs = {}
+        def double(c, engine):
+            lo, hi = STRETCHES[c]
+            for t in SCALAR_PLANES:
+                if engine == "scalar":
+                    nc.scalar.activation(out=window[t][:, lo:hi], in_=u_planes[c, t], func=ACT.Copy, scale=2.0)
+                else:
+                    nc.vector.tensor_scalar(out=window[t][:, lo:hi], in0=u_planes[c, t], scalar1=2.0, scalar2=None, op0=ALU.mult)
+
+        z_last = keep.tile([P, PLANES, P], F32, name="z_last")
+        first_two = {}
 
         def add_two(t):
-            pairs[t] = work([P, P], F32)
-            nc.vector.tensor_tensor(out=pairs[t][:], in0=terms[last, t][:, 0, :], in1=terms[last, t][:, 1, :], op=ALU.add)
+            first_two[t] = work([P, P], F32)
+            nc.vector.tensor_tensor(out=first_two[t][:], in0=terms[last, t][:, 0, :], in1=terms[last, t][:, 1, :], op=ALU.add)
 
         def add_third(t):
-            nc.vector.tensor_tensor(out=z_last[:, t, :], in0=pairs[t][:], in1=terms[last, t][:, 2, :], op=ALU.add)
+            nc.vector.tensor_tensor(out=z_last[:, t, :], in0=first_two[t][:], in1=terms[last, t][:, 2, :], op=ALU.add)
 
         add_two(0)
         add_two(1)
-        w23_plane = deal(s_raw[1], work([P, S], U8))
+        w23_dealt_scales = deal(raw_scales_23, work([P, S], U8))
         add_third(0)
         add_third(1)
         second_product(0)
@@ -299,84 +312,74 @@ def tile_picked_irls8_none_po_kernel(
         second_product(1)
         squash(1)
         add_third(3)
-        woven_z[last] = weave("vector", z_last[:], P)
+        woven_z[last] = weave("vector", z_last[:])
         second_product(last)
-        squash(last)
-        for t in (0, 1):
+        for t in range(PLANES):
             window[t] = work([P, S], F32)
-        for c in range(last + 1):
-            apply_gain(c)
+        apply_gain(0)
+        double(0, "vector")
+        double(1, "scalar")
+        apply_gain(1)
+        squash(last)
+        double(last, "scalar")
+        apply_gain(last)
 
-        out_scales = keep.tile([P, S], U8, name="out_scales", align_bytes=64)
-        out_rows = out_0.rearrange("(p t) s -> p t s", t=4)
-        out_words = words_view(out_1)
         pieces = S // P
-        moved_sigs, moved, woven_z2, products, results, woven_out = {}, {}, {}, {}, {}, {}
+        out_scales = keep.tile([P, S], U8, name="out_scales", align_bytes=64)
+        out_rows = out_0.rearrange("(p t) s -> p t s", t=PLANES)
+        out_words = words_view(out_1)
+        sigmoids, z2, woven_z2, products, results, woven_out = {}, {}, {}, {}, {}, {}
 
-        def entries_of(c):
-            return lists[3][:, c * P // 16 : (c + 1) * P // 16]
+        def fetch_on_scalar(c):
+            sigmoids[c] = work([P, len(SCALAR_PLANES), P], F32)
+            for i, t in enumerate(SCALAR_PLANES):
+                nc.scalar.activation(out=sigmoids[c][:, i, :], in_=window[t][:].indirect(entries(moves, c * P, (c + 1) * P)), func=ACT.Sigmoid)
 
-        def fetch_squashed(c):
-            entries = entries_of(c)
-            sig = work([P, 2, P], F32)
-            for t in (2, 3):
-                nc.scalar.activation(out=sig[:, t - 2, :], in_=window[t][:].indirect(entries), func=ACT.Sigmoid)
-            moved_sigs[c] = sig
-
-        def fetch_moved(c):
-            entries = entries_of(c)
-            sig = moved_sigs[c]
-            z2 = work([P, 4, P], BF16)
-            for t in (0, 1):
-                nc.vector.tensor_copy(out=z2[:, t, :], in_=window[t][:].indirect(entries))
-            for t in (2, 3):
-                centre(z2[:, t, :], sig[:, t - 2, :], t)
-            moved[c] = z2
-
-        def weave_moved(c):
-            woven_z2[c] = weave("scalar", moved[c][:], P)
+        def fetch_on_vector(c):
+            z2[c] = work([P, PLANES, P], BF16)
+            for t in VECTOR_PLANES:
+                nc.vector.tensor_copy(out=z2[c][:, t, :], in_=window[t][:].indirect(entries(moves, c * P, (c + 1) * P)))
+            for i, t in enumerate(SCALAR_PLANES):
+                nc.vector.tensor_scalar(out=z2[c][:, t, :], in0=sigmoids[c][:, i, :], scalar1=0.5, scalar2=twice_gain[:, t : t + 1],
+                                        op0=ALU.subtract, op1=ALU.mult)
 
         def last_product(c):
             codes, scales = quantise(woven_z2[c], P, "z2_scales%d" % c)
             products[c] = bank("b%d" % c)
-            for t in range(4):
-                product(products[c][:, P * t : P * (t + 1)], w3_codes, w23_plane, 4, t, codes[:], scales[:])
+            for t in range(PLANES):
+                product(products[c][:, P * t : P * (t + 1)], w3_codes, w23_dealt_scales, w3_row, t, codes[:], scales[:])
 
         def add_residual(c):
             cols = slice(c * P, (c + 1) * P)
-            result = work([P, 4, P], F32)
-            nc.vector.tensor_tensor(out=result[:], in0=products[c][:].rearrange("p (t n) -> p t n", t=4), in1=resid[:, :, cols], op=ALU.add)
-            nc.sync.dma_start(out=out_rows[:, :, cols], in_=result[:])
-            results[c] = result
+            results[c] = work([P, PLANES, P], F32)
+            nc.vector.tensor_tensor(out=results[c][:], in0=products[c][:].rearrange("p (t n) -> p t n", t=PLANES), in1=residual[:, :, cols], op=ALU.add)
+            nc.sync.dma_start(out=out_rows[:, :, cols], in_=results[c][:])
 
-        def weave_out(c):
-            woven_out[c] = weave("vector" if c == pieces - 1 else "scalar", results[c][:], P)
-
-        def planes_out(c):
+        def quantise_out(c):
             cols = slice(c * P, (c + 1) * P)
             nc.vector.quantize_mx(out=out_codes[:, cols].bitcast(FP8X4), scales=out_scales[:, cols], in_=woven_out[c][:].rearrange("p n t -> p (n t)"))
             if c % 2:
                 both = slice((c - 1) * P, (c + 1) * P)
                 nc.sync.dma_start(out=out_words[:, both], in_=out_codes[:, both].bitcast(I32))
 
-        fetch_squashed(0)
+        fetch_on_scalar(0)
         for c in range(pieces):
-            fetch_moved(c)
+            fetch_on_vector(c)
             if c > 0:
                 last_product(c - 1)
             if c + 1 < pieces:
-                fetch_squashed(c + 1)
-            weave_moved(c)
+                fetch_on_scalar(c + 1)
+            woven_z2[c] = weave("scalar", z2[c][:])
         add_residual(0)
         last_product(pieces - 1)
         for c in range(1, pieces):
             add_residual(c)
-            weave_out(c - 1)
+            woven_out[c - 1] = weave("scalar", results[c - 1][:])
         out_codes = work([P, S], U32)
-        planes_out(0)
-        weave_out(pieces - 1)
+        quantise_out(0)
+        woven_out[pieces - 1] = weave("vector", results[pieces - 1][:])
         for c in range(1, pieces):
-            planes_out(c)
+            quantise_out(c)
         for q in range(4):
             queue = nc.scalar if q % 2 else nc.sync
             queue.dma_start(out=out_2[0, 4 * q : 4 * q + 4, :].bitcast(I32), in_=out_scales[32 * q : 32 * q + 4, :].bitcast(I32))

@@ -22,10 +22,10 @@ PER_COLUMN = 16
 FLOPS = 3 * 2 * 512 * 512 * 512
 
 STRETCHES = ((0, 256), (256, 384), (384, 512))
-TURNED_PLANE = 0
+TURNED_PLANES = (0, 2)
 VECTOR_PLANES = (0, 1)
 SCALAR_PLANES = (2, 3)
-LAG = 2
+LAG = 3
 SLOTS = 44
 
 
@@ -133,7 +133,7 @@ def tile_picked_irls8_none_po_kernel(
         w2_codes = deal(raw_words[1], keep.tile([P, S], I32, name="w2_codes", align_bytes=64))
         w3_codes = deal(raw_words[2], keep.tile([P, S], I32, name="w3_codes", align_bytes=64))
         y = [keep.tile([P, S], F32, name="y%d" % t) for t in range(PLANES)]
-        minus_y = keep.tile([P, S], F32, name="minus_y")
+        minus_y = {t: keep.tile([P, S], F32, name="minus_y%d" % t) for t in TURNED_PLANES}
         for t in range(PLANES):
             banks = [bank("a%d" % t)]
             banks.append(bank("b0") if t == 0 else banks[0])
@@ -144,8 +144,8 @@ def tile_picked_irls8_none_po_kernel(
                     nc.scalar.copy(out=y[t][:, cols], in_=banks[i][:, cols])
             if t > 0:
                 nc.scalar.copy(out=y[t][:], in_=banks[0][:])
-            if t == TURNED_PLANE:
-                nc.scalar.activation(out=minus_y[:], in_=y[t][:], func=ACT.Copy, scale=-1.0)
+            if t in TURNED_PLANES:
+                nc.scalar.activation(out=minus_y[t][:], in_=y[t][:], func=ACT.Copy, scale=-1.0)
         nc.vector.tensor_scalar(out=twice_gain[:], in0=gain[:], scalar1=2.0, scalar2=None, op0=ALU.mult)
 
         units = [(c, t) for c in range(len(STRETCHES)) for t in range(PLANES)]
@@ -163,11 +163,11 @@ def tile_picked_irls8_none_po_kernel(
             for k in range(TERMS):
                 nc.vector.tensor_copy(out=x[:, k, :], in_=y[t][:].indirect(entries(neighbours[k], lo, hi)))
             fetched[c, t] = x
-            if t == TURNED_PLANE:
+            if t in TURNED_PLANES:
                 turned = [bank("b%d" % i, (P, TERMS * P)) for i in range(n // P)]
                 for k in range(TERMS):
                     for i, diff in enumerate(turned):
-                        nc.tensor.matmul(out=diff[:, k * P : (k + 1) * P], lhsT=minus_y[:, lo + i * P : lo + (i + 1) * P], rhs=identity[:],
+                        nc.tensor.matmul(out=diff[:, k * P : (k + 1) * P], lhsT=minus_y[t][:, lo + i * P : lo + (i + 1) * P], rhs=identity[:],
                                          start=True, stop=False, is_transpose=True)
                     for i, diff in enumerate(turned):
                         nc.tensor.matmul(out=diff[:, k * P : (k + 1) * P], lhsT=x[:, k, i * P : (i + 1) * P], rhs=identity[:],
@@ -186,7 +186,7 @@ def tile_picked_irls8_none_po_kernel(
                     nc.scalar.activation(out=stage[:, i, :], in_=parts[i], func=func, bias=bias)
                 parts = [stage[:, 0, :], stage[:, 1, :]]
             w = stage[:].rearrange("p i m -> p (i m)")
-            if t == TURNED_PLANE:
+            if t in TURNED_PLANES:
                 weights[c, t] = []
                 for i in range(n // P):
                     turned_back = bank("b%d" % (2 + i), (P, TERMS, P))
@@ -297,9 +297,10 @@ def tile_picked_irls8_none_po_kernel(
         def add_third(t):
             nc.vector.tensor_tensor(out=z_last[:, t, :], in0=first_two[t][:], in1=terms[last, t][:, 2, :], op=ALU.add)
 
+        w23_dealt_scales = deal(raw_scales_23, work([P, S], U8))
+        weigh(last, 1)
         add_two(0)
         add_two(1)
-        w23_dealt_scales = deal(raw_scales_23, work([P, S], U8))
         add_third(0)
         add_third(1)
         second_product(0)

from contextlib import ExitStack

import concourse.mybir as mybir
from concourse.masks import make_identity

F32 = mybir.dt.float32
BF16 = mybir.dt.bfloat16
I32 = mybir.dt.int32
U32 = mybir.dt.uint32
U16 = mybir.dt.uint16
U8 = mybir.dt.uint8
FP8X4 = mybir.dt.float8_e4m3fn_x4
ACT = mybir.ActivationFunctionType
ALU = mybir.AluOpType

P = 128
T = 2048
S = 512
PLANES = 4
TERMS = 3
PER_COLUMN = 16
FLOPS = 3 * 2 * 512 * 512 * 512

STRETCHES = ((0, 256), (256, 384), (384, 512))
TURNED_PLANES = (0, 2)
VECTOR_PLANES = (0, 1)
SCALAR_PLANES = (2, 3)
LAG = 3
SLOTS = 44


def tile_picked_irls8_none_po_kernel(
    tc, x_words, x_scales, w1_words, w1_scales, gn, w2_words, w2_scales, res, w3_words, w3_scales,
    offs, p1, p2, p3, mv, out_0, out_1, out_2,
):
    nc = tc.nc
    with ExitStack() as ctx:
        keep = ctx.enter_context(tc.tile_pool(name="keep", bufs=1))
        ring = ctx.enter_context(tc.tile_pool(name="ring", bufs=SLOTS))
        psum = ctx.enter_context(tc.psum_pool(name="psum", bufs=1))

        def work(shape, dtype):
            return ring.tile(shape, dtype, name="work", tag="work", align_bytes=64)

        def bank(tag, shape=(P, S)):
            return psum.tile(list(shape), F32, name="bank", tag=tag)

        def words_view(words):
            return words[0].rearrange("p n t -> p (n t)").bitcast(I32)

        def load_scales(tile, scales, row):
            for q in range(4):
                nc.sync.dma_start(out=tile[32 * q + row : 32 * q + row + 4, :].bitcast(I32), in_=scales[0, 4 * q : 4 * q + 4, :].bitcast(I32))

        def entries(held, lo, hi):
            return held[:, lo // PER_COLUMN : hi // PER_COLUMN]

        picks = keep.tile([P, S // PER_COLUMN], U16, name="picks")
        neighbours = [keep.tile([P, S // PER_COLUMN], U16, name="neighbours%d" % k) for k in range(TERMS)]
        moves = keep.tile([P, S // PER_COLUMN], U16, name="moves")
        table_words = keep.tile([P, T], I32, name="table_words", align_bytes=64)
        table_scales = keep.tile([P, T], U8, name="table_scales", align_bytes=64)
        raw_words = [keep.tile([P, S], I32, name="raw_words%d" % i, align_bytes=64) for i in range(3)]
        raw_scales_1 = keep.tile([P, S], U8, name="raw_scales_1", align_bytes=64)
        raw_scales_23 = keep.tile([P, S], U8, name="raw_scales_23", align_bytes=64)
        w3_row = 4
        gain = keep.tile([P, PLANES], F32, name="gain")
        twice_gain = keep.tile([P, PLANES], F32, name="twice_gain")
        residual = keep.tile([P, PLANES, S], F32, name="residual")
        warm = keep.tile([P, 2], F32, name="warm")
        identity = keep.tile([P, P], F32, name="identity")

        nc.vector.memset(table_scales[:].bitcast(I32), 0)
        nc.gpsimd.memset(raw_scales_1[:].bitcast(I32), 0)
        nc.gpsimd.memset(warm[:, 0:1], 1.0)
        nc.scalar.activation(out=warm[:, 1:2], in_=warm[:, 0:1], func=ACT.Abs_reciprocal_sqrt)
        nc.gpsimd.memset(raw_scales_23[:].bitcast(I32), 0)
        make_identity(nc, identity[:])

        nc.sync.dma_start(picks[:], offs)
        nc.sync.dma_start(out=raw_words[0][:], in_=words_view(w1_words))
        load_scales(table_scales, x_scales, 0)
        nc.sync.dma_start(out=table_words[:], in_=words_view(x_words))
        load_scales(raw_scales_1, w1_scales, 0)
        nc.sync.dma_start(neighbours[0][:], p1)
        nc.sync.dma_start(out=raw_words[1][:], in_=words_view(w2_words))
        nc.sync.dma_start(out=raw_words[2][:], in_=words_view(w3_words))
        nc.sync.dma_start(neighbours[1][:], p2)
        nc.sync.dma_start(neighbours[2][:], p3)
        nc.sync.dma_start(out=gain[:], in_=gn.rearrange("(p t) o -> p (t o)", t=PLANES))
        load_scales(raw_scales_23, w2_scales, 0)
        load_scales(raw_scales_23, w3_scales, w3_row)
        nc.sync.dma_start(moves[:], mv)
        nc.sync.dma_start(out=residual[:], in_=res.rearrange("(p t) s -> p t s", t=PLANES))

        def deal(raw, dealt):
            nc.vector.tensor_copy(out=dealt[:].rearrange("p (t m) -> p m t", t=PLANES), in_=raw[:].rearrange("p (m t) -> p m t", t=PLANES))
            return dealt

        def product(out, w_codes, w_scales, row, t, codes, scales):
            m = slice(P * t, P * (t + 1))
            nc.tensor.matmul_mx(out=out, lhsT=w_codes[:, m].bitcast(FP8X4), lhsT_scale=w_scales[row:P, m],
                                rhs=codes.bitcast(FP8X4), rhs_scale=scales, start=True, stop=True)

        def weave(engine, planes):
            woven = work([P, P, PLANES], BF16)
            out = woven[:].rearrange("p (c i) t -> p c t i", i=4)
            in_ = planes.rearrange("p t (c i) -> p c t i", i=4)
            if engine == "scalar":
                nc.scalar.activation(out=out, in_=in_, func=ACT.Copy)
            else:
                nc.vector.tensor_copy(out=out, in_=in_)
            return woven

        def quantise(woven, n, name):
            codes = work([P, n], U32)
            scales = keep.tile([P, n], U8, name=name, align_bytes=64)
            nc.vector.quantize_mx(out=codes[:].bitcast(FP8X4), scales=scales[:], in_=woven[:].rearrange("p n t -> p (n t)"))
            return codes, scales

        def pick_words(lo, hi):
            words = work([P, hi - lo], U32)
            nc.vector.tensor_copy(out=words[:], in_=table_words[:].bitcast(U32).indirect(entries(picks, lo, hi)))
            return words

        half = S // 2
        w1_codes = deal(raw_words[0], work([P, S], I32))
        picked_scales = work([P, S], U8)
        nc.vector.tensor_copy(out=picked_scales[:], in_=table_scales[:].indirect(picks[:]))
        picked = [pick_words(0, half)]
        w1_dealt_scales = deal(raw_scales_1, work([P, S], U8))
        picked.append(pick_words(half, S))
        w2_codes = deal(raw_words[1], keep.tile([P, S], I32, name="w2_codes", align_bytes=64))
        w3_codes = deal(raw_words[2], keep.tile([P, S], I32, name="w3_codes", align_bytes=64))
        y = [keep.tile([P, S], F32, name="y%d" % t) for t in range(PLANES)]
        minus_y = {t: keep.tile([P, S], F32, name="minus_y%d" % t) for t in TURNED_PLANES}
        for t in range(PLANES):
            banks = [bank("a%d" % t)]
            banks.append(bank("b0") if t == 0 else banks[0])
            for i in range(2):
                cols = slice(i * half, (i + 1) * half)
                product(banks[i][:, cols], w1_codes, w1_dealt_scales, 0, t, picked[i][:], picked_scales[:, cols])
                if t == 0:
                    nc.scalar.copy(out=y[t][:, cols], in_=banks[i][:, cols])
            if t > 0:
                nc.scalar.copy(out=y[t][:], in_=banks[0][:])
            if t in TURNED_PLANES:
                nc.scalar.activation(out=minus_y[t][:], in_=y[t][:], func=ACT.Copy, scale=-1.0)
        nc.vector.tensor_scalar(out=twice_gain[:], in0=gain[:], scalar1=2.0, scalar2=None, op0=ALU.mult)

        units = [(c, t) for c in range(len(STRETCHES)) for t in range(PLANES)]
        last = len(STRETCHES) - 1
        fetched, weights, terms, sums, word_pairs, woven_z = {}, {}, {}, {}, {}, {}

        def in_halves(flat):
            middle = flat.shape[1] // 2
            return [flat[:, :middle], flat[:, middle:]]

        def differences(c, t):
            lo, hi = STRETCHES[c]
            n = hi - lo
            x = work([P, TERMS, n], F32)
            for k in range(TERMS):
                nc.vector.tensor_copy(out=x[:, k, :], in_=y[t][:].indirect(entries(neighbours[k], lo, hi)))
            fetched[c, t] = x
            if t in TURNED_PLANES:
                turned = [bank("b%d" % i, (P, TERMS * P)) for i in range(n // P)]
                for k in range(TERMS):
                    for i, diff in enumerate(turned):
                        nc.tensor.matmul(out=diff[:, k * P : (k + 1) * P], lhsT=minus_y[t][:, lo + i * P : lo + (i + 1) * P], rhs=identity[:],
                                         start=True, stop=False, is_transpose=True)
                    for i, diff in enumerate(turned):
                        nc.tensor.matmul(out=diff[:, k * P : (k + 1) * P], lhsT=x[:, k, i * P : (i + 1) * P], rhs=identity[:],
                                         start=False, stop=True, is_transpose=True)
                return [diff[:] for diff in turned] if n > P else in_halves(turned[0][:])
            d = work([P, TERMS, n], F32)
            nc.vector.tensor_tensor(out=d[:, 0:2, :], in0=x[:, 0:2, :], in1=y[t][:, lo:hi].unsqueeze(1).to_broadcast([P, 2, n]), op=ALU.subtract)
            nc.vector.tensor_tensor(out=d[:, 2, :], in0=x[:, 2, :], in1=y[t][:, lo:hi], op=ALU.subtract)
            return in_halves(d[:].rearrange("p k n -> p (k n)"))

        def robust_weights(c, t, parts):
            n = STRETCHES[c][1] - STRETCHES[c][0]
            for func, bias in ((ACT.Square, 0.0), (ACT.Abs_reciprocal_sqrt, 1.0), (ACT.Square, 0.0)):
                stage = work([P, 2, TERMS * n // 2], F32)
                for i in range(2):
                    nc.scalar.activation(out=stage[:, i, :], in_=parts[i], func=func, bias=bias)
                parts = [stage[:, 0, :], stage[:, 1, :]]
            w = stage[:].rearrange("p i m -> p (i m)")
            if t in TURNED_PLANES:
                weights[c, t] = []
                for i in range(n // P):
                    turned_back = bank("b%d" % (2 + i), (P, TERMS, P))
                    for k in range(TERMS):
                        nc.tensor.transpose(turned_back[:, k, :], w[:, (TERMS * i + k) * P : (TERMS * i + k + 1) * P], identity[:])
                    weights[c, t].append(turned_back[:])
            else:
                weights[c, t] = [w.rearrange("p (k n) -> p k n", k=TERMS)]

        def weigh(c, t):
            lo, hi = STRETCHES[c]
            r = work([P, TERMS, hi - lo], F32)
            terms[c, t] = r
            width = (hi - lo) // len(weights[c, t])
            for i, w in enumerate(weights[c, t]):
                cols = slice(i * width, (i + 1) * width)
                nc.vector.scalar_tensor_tensor(out=r[:, :, cols], in0=fetched[c, t][:, :, cols], scalar=gain[:, t : t + 1], in1=w,
                                               op0=ALU.mult, op1=ALU.mult)
            if c == last:
                return
            for j in range(lo, hi, P):
                if t == 0:
                    sums[j] = bank("a%d" % (j // P))
                for k in range(TERMS):
                    nc.tensor.matmul(out=sums[j][:, P * t : P * (t + 1)], lhsT=r[:, k, j - lo : j - lo + P], rhs=identity[:],
                                     start=(k == 0), stop=(k == TERMS - 1), is_transpose=True)

        def round_sums(c):
            lo, hi = STRETCHES[c]
            n = hi - lo
            rounded = work([P, n // P, 2, P, 2], BF16)
            for i in range(n // P):
                nc.scalar.activation(out=rounded[:, i], in_=sums[lo + i * P][:].rearrange("p (u e m) -> p u m e", u=2, e=2), func=ACT.Copy)
            as_words = rounded[:].rearrange("p i u m e -> p (i u m e)").bitcast(F32)
            word_pairs[c] = bank("a3", (P, 2 * n))
            for i in range(n // P):
                for u in range(2):
                    nc.tensor.transpose(word_pairs[c][:, u * n + i * P : u * n + (i + 1) * P],
                                        as_words[:, (2 * i + u) * P : (2 * i + u + 1) * P], identity[:])

        def join_pairs(c):
            n = STRETCHES[c][1] - STRETCHES[c][0]
            woven_z[c] = work([P, n, PLANES], BF16)
            nc.scalar.copy(out=woven_z[c][:].rearrange("p n t -> p (n t)").bitcast(F32).rearrange("p (n u) -> p n u", u=2),
                           in_=word_pairs[c][:].rearrange("p (u n) -> p n u", u=2))

        for step, (c, t) in enumerate(units):
            parts = differences(c, t)
            if step >= LAG:
                weigh(*units[step - LAG])
            robust_weights(c, t, parts)
            for done in range(last):
                weighed_at = PLANES * done + PLANES - 1 + LAG
                if step == weighed_at:
                    round_sums(done)
                if step == weighed_at + 1:
                    join_pairs(done)

        warm_sigmoid = work([P, 1], F32)
        nc.scalar.activation(out=warm_sigmoid[:], in_=warm[:, 0:1], func=ACT.Sigmoid)

        u_banks = (("b0", "b0", "b1", "b1"), ("b2",) * PLANES, ("b3", "a0", "a1", "a2"))
        u_planes, u_first_two, squashed, window = {}, {}, {}, {}

        def second_product(c):
            n = STRETCHES[c][1] - STRETCHES[c][0]
            codes, scales = quantise(woven_z[c], n, "z_scales%d" % c)
            banks = {}
            for t in range(PLANES):
                tag = u_banks[c][t]
                place = u_banks[c][:t].count(tag) * n
                if tag not in banks:
                    banks[tag] = bank(tag)
                u_planes[c, t] = banks[tag][:, place : place + n]
                product(u_planes[c, t], w2_codes, w23_dealt_scales, 0, t, codes[:], scales[:])
            if c < last:
                u_first_two[c] = banks[u_banks[c][0]][:, 0 : 2 * n]

        def squash(c):
            lo, hi = STRETCHES[c]
            squashed[c] = work([P, len(VECTOR_PLANES), hi - lo], F32)
            if c < last:
                nc.scalar.activation(out=squashed[c][:].rearrange("p t n -> p (t n)"), in_=u_first_two[c], func=ACT.Tanh)
            else:
                for t in VECTOR_PLANES:
                    nc.scalar.activation(out=squashed[c][:, t, :], in_=u_planes[c, t], func=ACT.Tanh)

        def apply_gain(c):
            lo, hi = STRETCHES[c]
            for t in VECTOR_PLANES:
                nc.vector.tensor_scalar(out=window[t][:, lo:hi], in0=squashed[c][:, t, :], scalar1=gain[:, t : t + 1], scalar2=None, op0=ALU.mult)

        def double(c, engine):
            lo, hi = STRETCHES[c]
            for t in SCALAR_PLANES:
                if engine == "scalar":
                    nc.scalar.activation(out=window[t][:, lo:hi], in_=u_planes[c, t], func=ACT.Copy, scale=2.0)
                else:
                    nc.vector.tensor_scalar(out=window[t][:, lo:hi], in0=u_planes[c, t], scalar1=2.0, scalar2=None, op0=ALU.mult)

        z_last = keep.tile([P, PLANES, P], F32, name="z_last")
        first_two = {}

        def add_two(t):
            first_two[t] = work([P, P], F32)
            nc.vector.tensor_tensor(out=first_two[t][:], in0=terms[last, t][:, 0, :], in1=terms[last, t][:, 1, :], op=ALU.add)

        def add_third(t):
            nc.vector.tensor_tensor(out=z_last[:, t, :], in0=first_two[t][:], in1=terms[last, t][:, 2, :], op=ALU.add)

        w23_dealt_scales = deal(raw_scales_23, work([P, S], U8))
        weigh(last, 1)
        add_two(0)
        add_two(1)
        add_third(0)
        add_third(1)
        second_product(0)
        squash(0)
        weigh(last, 2)
        weigh(last, 3)
        add_two(2)
        add_two(3)
        add_third(2)
        second_product(1)
        squash(1)
        add_third(3)
        woven_z[last] = weave("vector", z_last[:])
        second_product(last)
        for t in range(PLANES):
            window[t] = work([P, S], F32)
        apply_gain(0)
        double(0, "vector")
        double(1, "scalar")
        apply_gain(1)
        squash(last)
        double(last, "scalar")
        apply_gain(last)

        pieces = S // P
        out_scales = keep.tile([P, S], U8, name="out_scales", align_bytes=64)
        out_rows = out_0.rearrange("(p t) s -> p t s", t=PLANES)
        out_words = words_view(out_1)
        sigmoids, z2, woven_z2, products, results, woven_out = {}, {}, {}, {}, {}, {}

        def fetch_on_scalar(c):
            sigmoids[c] = work([P, len(SCALAR_PLANES), P], F32)
            for i, t in enumerate(SCALAR_PLANES):
                nc.scalar.activation(out=sigmoids[c][:, i, :], in_=window[t][:].indirect(entries(moves, c * P, (c + 1) * P)), func=ACT.Sigmoid)

        def fetch_on_vector(c):
            z2[c] = work([P, PLANES, P], BF16)
            for t in VECTOR_PLANES:
                nc.vector.tensor_copy(out=z2[c][:, t, :], in_=window[t][:].indirect(entries(moves, c * P, (c + 1) * P)))
            for i, t in enumerate(SCALAR_PLANES):
                nc.vector.tensor_scalar(out=z2[c][:, t, :], in0=sigmoids[c][:, i, :], scalar1=0.5, scalar2=twice_gain[:, t : t + 1],
                                        op0=ALU.subtract, op1=ALU.mult)

        def last_product(c):
            codes, scales = quantise(woven_z2[c], P, "z2_scales%d" % c)
            products[c] = bank("b%d" % c)
            for t in range(PLANES):
                product(products[c][:, P * t : P * (t + 1)], w3_codes, w23_dealt_scales, w3_row, t, codes[:], scales[:])

        def add_residual(c):
            cols = slice(c * P, (c + 1) * P)
            results[c] = work([P, PLANES, P], F32)
            nc.vector.tensor_tensor(out=results[c][:], in0=products[c][:].rearrange("p (t n) -> p t n", t=PLANES), in1=residual[:, :, cols], op=ALU.add)
            nc.sync.dma_start(out=out_rows[:, :, cols], in_=results[c][:])

        def quantise_out(c):
            cols = slice(c * P, (c + 1) * P)
            nc.vector.quantize_mx(out=out_codes[:, cols].bitcast(FP8X4), scales=out_scales[:, cols], in_=woven_out[c][:].rearrange("p n t -> p (n t)"))
            if c % 2:
                both = slice((c - 1) * P, (c + 1) * P)
                nc.sync.dma_start(out=out_words[:, both], in_=out_codes[:, both].bitcast(I32))

        fetch_on_scalar(0)
        for c in range(pieces):
            fetch_on_vector(c)
            if c > 0:
                last_product(c - 1)
            if c + 1 < pieces:
                fetch_on_scalar(c + 1)
            woven_z2[c] = weave("scalar", z2[c][:])
        add_residual(0)
        last_product(pieces - 1)
        for c in range(1, pieces):
            add_residual(c)
            woven_out[c - 1] = weave("scalar", results[c - 1][:])
        out_codes = work([P, S], U32)
        quantise_out(0)
        woven_out[pieces - 1] = weave("vector", results[pieces - 1][:])
        for c in range(1, pieces):
            quantise_out(c)
        for q in range(4):
            queue = nc.scalar if q % 2 else nc.sync
            queue.dma_start(out=out_2[0, 4 * q : 4 * q + 4, :].bitcast(I32), in_=out_scales[32 * q : 32 * q + 4, :].bitcast(I32))
